import numpy as np
import ml_dtypes


def mxq(x, axis, fmt="e4m3"):
    dtype, down = {"e4m3": (ml_dtypes.float8_e4m3fn, 7), "e5m2": (ml_dtypes.float8_e5m2, 14)}[fmt]
    v = np.moveaxis(np.asarray(x, np.float32).astype(ml_dtypes.bfloat16).astype(np.float64), axis, -1)
    blocks = v.reshape(v.shape[:-1] + (-1, 32))
    amax = np.abs(blocks).max(-1, keepdims=True)
    byte = np.maximum(np.where(amax > 0, np.frexp(amax)[1] - 1 + 127, 0) - down, 1)
    scale = np.exp2(byte - 127.0)
    codes = (blocks / scale).astype(np.float32).astype(dtype).astype(np.float64)
    return np.moveaxis((codes * scale).reshape(v.shape), -1, axis)


WIDE = False


def mx_kscale(k):
    if not WIDE:
        return np.ones(k)
    levels = np.array([24, -24, 12, -12, 0])
    if k % 512:
        return np.exp2(np.random.permutation(np.resize(levels, k // 32))).repeat(32)
    a = np.empty((k // 512, 16))
    for p in range(k // 512):
        a[p, :8] = np.random.permutation(np.resize(levels, 8))
        for g in range(8):
            far = levels[np.abs(levels - a[p, g]) >= 10]
            a[p, g + 8] = far[np.random.randint(len(far))]
    return np.exp2(a.ravel()).repeat(32)


def f64(x):
    return np.asarray(x).astype(np.float64)


def striped(idx):
    return np.tile(idx.reshape(-1, 16).T, (8, 1)).astype(np.uint16)


def unstriped(offs):
    return offs[:16].T.reshape(-1).astype(np.int64)


E2M1 = np.array([0.0, 0.5, 1.0, 1.5, 2.0, 3.0, 4.0, 6.0, -0.0, -0.5, -1.0, -1.5, -2.0, -3.0, -4.0, -6.0])


def pack_weight(w, fmt):
    k, n = w.shape
    w = f64(np.asarray(w, np.float32).astype(ml_dtypes.bfloat16)).reshape(k // 32, 32, n)
    amax = np.abs(w).max(1)
    if fmt == "e4m3":
        byte = np.frexp(amax)[1] - 1 + 127 - 7
    else:
        mant, ex = np.frexp(amax / 6.0)
        byte = np.where(mant > 0.5, ex, ex - 1) + 127
    byte = np.clip(np.where(amax > 0, byte, 1), 1, 254)
    scaled = (w * np.exp2(127.0 - byte)[:, None, :]).reshape(k, n).astype(np.float32)
    by_word = np.ascontiguousarray(scaled.reshape(k // 512, 128, 4, n).transpose(0, 1, 3, 2))
    if fmt == "e4m3":
        words = by_word.astype(ml_dtypes.float8_e4m3fn).view(np.uint8)
    else:
        c = by_word.astype(ml_dtypes.float4_e2m1fn).view(np.uint8) & 0xF
        words = (c[..., 0::2] | (c[..., 1::2] << 4)).reshape(k // 512, 128, 2 * n)
    return np.ascontiguousarray(words), np.ascontiguousarray(byte.astype(np.uint8).reshape(k // 512, 16, n))


def unpack_weight(words, scales, fmt):
    g, _, n = scales.shape
    words = np.ascontiguousarray(words).reshape(g, 128, n, -1)
    if fmt == "e4m3":
        vals = words.view(ml_dtypes.float8_e4m3fn).astype(np.float64)
    else:
        nib = np.empty((g, 128, n, 4), np.uint8)
        nib[..., 0::2] = words & 0xF
        nib[..., 1::2] = words >> 4
        vals = E2M1[nib]
    vals = vals * np.repeat(np.exp2(scales.astype(np.float64) - 127.0), 8, axis=1)[..., None]
    return vals.transpose(0, 1, 3, 2).reshape(g * 512, n)


def planes(y):
    n, m = y.shape
    v = y.astype(np.float32).astype(ml_dtypes.bfloat16).astype(np.float64).reshape(n // 32, 32, m)
    top = np.abs(v).max(1)
    byte = np.clip(np.where(top > 0, np.frexp(top)[1] - 1 + 127 - 7, 1), 1, 254)
    codes = (v * np.exp2(127.0 - byte)[:, None, :]).reshape(n, m).astype(np.float32).astype(ml_dtypes.float8_e4m3fn).view(np.uint8)
    words = codes.reshape(n // 512, 128, 4, m).transpose(0, 1, 3, 2)
    return np.ascontiguousarray(words), np.ascontiguousarray(byte.astype(np.uint8).reshape(n // 512, 16, m))


def silu(f):
    return f / (1.0 + np.exp(-np.maximum(f, -700.0)))


K, R, N, T, J = 512, 512, 512, 2048, 1024


def setup_inputs():
    n = np.random.standard_normal
    s = mx_kscale(K)[:, None]
    u = mx_kscale(R)[:, None]
    p_tab = pack_weight(n((K, T)) * s, "e4m3")
    p_ws = pack_weight(n((K, R)) / np.sqrt(2 * K) / s, "e4m3")
    p_wt = pack_weight(n((K, R)) / np.sqrt(2 * K) / s, "e4m3")
    return {
        "tab_words": p_tab[0],
        "tab_scales": p_tab[1],
        "ws_words": p_ws[0],
        "ws_scales": p_ws[1],
        "wt_words": p_wt[0],
        "wt_scales": p_wt[1],
        "sm": (np.random.uniform(0.5, 2.0, R) * u[:, 0]).astype(np.float32),
        "wd": (n((R, N)) / np.sqrt(R) / u).astype(np.float32),
        "wgo": np.tile(np.random.uniform(0.5, 2.0, J), (128, 1)).astype(np.float32),
        "offs": striped(np.random.permutation(T)[:J]),
        "offs2": striped(np.random.permutation(T)[:J]),
    }


def reference(tab_words, tab_scales, ws_words, ws_scales, wt_words, wt_scales, sm, wd, wgo, offs, offs2):
    idx = unstriped(offs)
    idx2 = unstriped(offs2)
    tab_ = unpack_weight(tab_words, tab_scales, "e4m3")[:, idx]
    tabb_ = unpack_weight(tab_words, tab_scales, "e4m3")[:, idx2]
    ws_ = unpack_weight(ws_words, ws_scales, "e4m3")
    wt_ = unpack_weight(wt_words, wt_scales, "e4m3")
    a = ws_.T @ tab_ + wt_.T @ tabb_
    h = f64(sm)[:, None] * silu(a)
    h_ = mxq(h, 0, "e4m3")
    wd_ = mxq(f64(wd), 0, "e4m3")
    y = wd_.T @ h_
    out = np.zeros((N, T))
    out[:, idx2] = f64(wgo)[0] * (y)
    return (out,) + planes(out)

@@ -1,0 +1,228 @@
+from contextlib import ExitStack
+
+import concourse.mybir as mybir
+
+K, R, N, T, J = 512, 512, 512, 2048, 1024
+FLOPS = 2 * J * (2 * K * R + R * N)
+
+F32 = mybir.dt.float32
+BF16 = mybir.dt.bfloat16
+I32 = mybir.dt.int32
+U32 = mybir.dt.uint32
+U16 = mybir.dt.uint16
+U8 = mybir.dt.uint8
+FP8X4 = mybir.dt.float8_e4m3fn_x4
+SILU = mybir.ActivationFunctionType.Silu
+COPY = mybir.ActivationFunctionType.Copy
+MULT = mybir.AluOpType.mult
+
+P = 128
+PACK = 4
+EDGES = 256
+CHUNKS = J // EDGES
+LIST_COLS = EDGES // 16
+NODES = 256
+PIECES = T // NODES
+
+
+def tile_list_msg_silu_noneP_kernel(
+    tc, tab_words, tab_scales, ws_words, ws_scales, wt_words, wt_scales, sm, wd, wgo, offs, offs2, out_0, out_1, out_2
+):
+    nc = tc.nc
+    with ExitStack() as ctx:
+        keep = ctx.enter_context(tc.tile_pool(name="keep", bufs=1))
+        ring = ctx.enter_context(tc.tile_pool(name="ring", bufs=2))
+        psum = ctx.enter_context(tc.psum_pool(name="psum", bufs=2))
+
+        def load_scale_rows(queue, plane, first, rows):
+            for quad in range(4):
+                queue.dma_start(
+                    out=plane[32 * quad + first : 32 * quad + first + 4, :].bitcast(I32),
+                    in_=rows[0, 4 * quad : 4 * quad + 4, :].bitcast(I32),
+                )
+
+        def words_of(packed):
+            return packed[0].rearrange("p c i -> p (c i)").bitcast(I32)
+
+        tab_plane = keep.tile([P, T], U8, name="tab_plane", align_bytes=64)
+        w_plane = keep.tile([P, R], U8, name="w_plane", tag="after_weights", align_bytes=64)
+        nc.vector.memset(w_plane[:].bitcast(I32), 0)
+        nc.vector.memset(tab_plane[:].bitcast(I32), 0)
+
+        src_list = keep.tile([P, J // 16], U16, name="src_list")
+        dst_list = keep.tile([P, J // 16], U16, name="dst_list")
+        sm_sb = keep.tile([P, PACK], F32, name="sm_sb")
+        nc.sync.dma_start(src_list[:], offs)
+        tab_sb = keep.tile([P, T], I32, name="tab_sb", tag="after_gathers", align_bytes=64)
+        nc.sync.dma_start(out=tab_sb[:], in_=words_of(tab_words))
+        w_raw = keep.tile([P, 2, R], I32, name="w_raw", tag="after_words")
+        nc.sync.dma_start(out=w_raw[:, 0, :], in_=words_of(ws_words))
+        nc.sync.dma_start(out=w_raw[:, 1, :], in_=words_of(wt_words))
+        nc.sync.dma_start(dst_list[:], offs2)
+        load_scale_rows(nc.sync, tab_plane, 0, tab_scales)
+        load_scale_rows(nc.sync, w_plane, 0, ws_scales)
+        load_scale_rows(nc.gpsimd, w_plane, 4, wt_scales)
+        nc.gpsimd.dma_start(out=sm_sb[:], in_=sm.rearrange("(p t) -> p t", t=PACK))
+
+        pages = {}
+        for i in (0, 1, 2):
+            pages[i] = keep.tile([P, T], F32, name="page%d" % i)
+            nc.vector.memset(pages[i][:].bitcast(I32), 0)
+
+        w_codes = keep.tile([P, 2, PACK, P], I32, name="w_codes", align_bytes=64)
+        w_scales = keep.tile([P, PACK, P], U8, name="w_scales", align_bytes=64)
+        nc.vector.tensor_copy(
+            out=w_codes[:].rearrange("p w t m -> p w m t"), in_=w_raw[:].rearrange("p w (m t) -> p w m t", t=PACK)
+        )
+        nc.vector.tensor_copy(
+            out=w_scales[:].rearrange("p t m -> p m t"), in_=w_plane[:].rearrange("p (m t) -> p m t", t=PACK)
+        )
+
+        wd_raw = keep.tile([P, PACK, N], F32, name="wd_raw", tag="after_words")
+        nc.sync.dma_start(out=wd_raw[:], in_=wd.rearrange("(p j) n -> p j n", j=PACK))
+
+        lists = (src_list, dst_list)
+        picked_words, picked_scales = {}, {}
+
+        def gather(window, dtype, picked, first, count, tag):
+            got = keep.tile([P, 2, count * EDGES], dtype, name="%s_%d" % (tag, first), tag=tag, align_bytes=64)
+            for side in (0, 1):
+                nc.vector.tensor_copy(
+                    got[:, side, :], window.indirect(lists[side][:, first * LIST_COLS : (first + count) * LIST_COLS])
+                )
+                for c in range(count):
+                    picked[first + c, side] = got[:, side, c * EDGES : (c + 1) * EDGES]
+
+        def gather_words(first, count, tag):
+            gather(tab_sb[:].bitcast(U32), U32, picked_words, first, count, tag)
+
+        def gather_scales(first, count, tag):
+            gather(tab_plane[:], U8, picked_scales, first, count, tag)
+
+        wd_codes, wd_scales = {}, {}
+
+        def prepare_wd(half):
+            grouped = keep.tile([P, 2, P, PACK], BF16, name="wd_grouped%d" % half, align_bytes=64)
+            nc.scalar.copy(
+                out=grouped[:].rearrange("p i m j -> p m j i"),
+                in_=wd_raw[:].rearrange("p j (m i) -> p m j i", i=PACK)[:, :, :, 2 * half : 2 * half + 2],
+            )
+            codes = keep.tile([P, 2 * P], U32, name="wd_codes%d" % half, align_bytes=64)
+            scales = keep.tile([P, 2 * P], U8, name="wd_scales%d" % half, align_bytes=64)
+            nc.vector.quantize_mx(
+                out=codes[:].bitcast(FP8X4), scales=scales[:], in_=grouped[:].rearrange("p i m j -> p (i m j)")
+            )
+            for i in (0, 1):
+                wd_codes[2 * half + i] = codes[:, i * P : (i + 1) * P]
+                wd_scales[2 * half + i] = scales[:, i * P : (i + 1) * P]
+
+        h_codes = keep.tile([P, J], U32, name="h_codes", align_bytes=64)
+        h_scales = keep.tile([P, J], U8, name="h_scales", align_bytes=64)
+
+        def hidden(c, tag):
+            act = ring.tile([P, PACK, EDGES], F32, name="act")
+            for pair in (0, 1):
+                bank = psum.tile([P, 2, EDGES], F32, name="a_bank%d" % pair)
+                for u in (0, 1):
+                    t = 2 * pair + u
+                    for side in (0, 1):
+                        nc.tensor.matmul_mx(
+                            out=bank[:, u, :],
+                            lhsT=w_codes[:, side, t, :].bitcast(FP8X4),
+                            lhsT_scale=w_scales[4 * side :, t, :],
+                            rhs=picked_words[c, side].bitcast(FP8X4),
+                            rhs_scale=picked_scales[c, side],
+                            start=(side == 0),
+                            stop=(side == 1),
+                        )
+                nc.scalar.activation(act[:, 2 * pair : 2 * pair + 2, :], bank[:], SILU)
+            h_rows = keep.tile([P, PACK, EDGES], BF16, name="h_rows%d" % c, tag="after_h_rows%d" % c)
+            for t in range(PACK):
+                nc.scalar.activation(h_rows[:, t, :], act[:, t, :], COPY, scale=sm_sb[:, t : t + 1])
+            h_grouped = keep.tile([P, EDGES, PACK], BF16, name="h_grouped%d" % c, tag=tag, align_bytes=64)
+            nc.scalar.copy(
+                out=h_grouped[:].rearrange("p (e f) t -> p e t f", f=4),
+                in_=h_rows[:].rearrange("p t (e f) -> p e t f", f=4),
+            )
+            cols = slice(c * EDGES, (c + 1) * EDGES)
+            nc.vector.quantize_mx(
+                out=h_codes[:, cols].bitcast(FP8X4),
+                scales=h_scales[:, cols],
+                in_=h_grouped[:].rearrange("p e t -> p (e t)"),
+            )
+
+        def messages(planes, first, count, bank_name, tag):
+            cols = slice(first, first + count)
+            bank = psum.tile([P, len(planes), count], F32, name=bank_name)
+            for u, i in enumerate(planes):
+                nc.tensor.matmul_mx(
+                    out=bank[:, u, :],
+                    lhsT=wd_codes[i].bitcast(FP8X4),
+                    lhsT_scale=wd_scales[i],
+                    rhs=h_codes[:, cols].bitcast(FP8X4),
+                    rhs_scale=h_scales[:, cols],
+                    start=True,
+                    stop=True,
+                )
+            y_sb = keep.tile([P, len(planes), count], F32, name="y%d_%d" % (planes[0], first), tag=tag)
+            nc.scalar.copy(out=y_sb[:], in_=bank[:])
+            for u, i in enumerate(planes):
+                nc.vector.tensor_tensor(
+                    pages[i][:].indirect(dst_list[:, first // 16 : (first + count) // 16]),
+                    y_sb[:, u, :],
+                    wgo_sb[:, cols],
+                    MULT,
+                )
+
+        gather_words(0, 1, "words_first")
+        gather_scales(0, 1, "after_first_sums")
+        gather_scales(1, 1, "scales_second")
+        gather_words(1, 2, "after_weights")
+        prepare_wd(0)
+        hidden(0, "after_first_h")
+        wgo_sb = keep.tile([P, J], F32, name="wgo_sb", tag="words_first", align_bytes=64)
+        nc.sync.dma_start(out=wgo_sb[:], in_=wgo)
+        gather_scales(2, 2, "after_first_sums")
+        gather_words(3, 1, "after_first_h")
+        pages[3] = keep.tile([P, T], F32, name="page3", tag="after_gathers", align_bytes=64)
+        for quarter in range(4):
+            nc.gpsimd.memset(pages[3][:, quarter * 512 : (quarter + 1) * 512], 0.0)
+        messages((0, 1), 0, EDGES, "y_pair", "y_pair0")
+        prepare_wd(1)
+        for c in range(1, CHUNKS):
+            hidden(c, "h_grouped%d" % c)
+            messages((2,), (c - 1) * EDGES, EDGES, "y_one", "after_h_rows%d" % c)
+            messages((0, 1), c * EDGES, EDGES, "y_pair", "y_pair%d" % c)
+        messages((2,), (CHUNKS - 1) * EDGES, EDGES, "y_one", "y_third_last")
+        messages((3,), 0, 2 * EDGES, "y_one", "y_fourth0")
+        messages((3,), 2 * EDGES, 2 * EDGES, "y_one", "y_fourth1")
+
+        out_rows = out_0.rearrange("(p i) t -> i p t", i=PACK)
+        pairs = [keep.tile([P, 2, NODES, 2], BF16, name="pairs%d" % k) for k in range(PIECES)]
+        for i in range(PACK):
+            nc.sync.dma_start(out=out_rows[i], in_=pages[i][:])
+            if i < PACK - 1:
+                for k in range(PIECES):
+                    nc.scalar.copy(out=pairs[k][:, i // 2, :, i % 2], in_=pages[i][:, k * NODES : (k + 1) * NODES])
+        out_scales = keep.tile([P, T], U8, name="out_scales", align_bytes=64)
+        out_words = out_1[0].rearrange("p c i -> p (c i)").bitcast(I32)
+        for k in range(PIECES):
+            cols = slice(k * NODES, (k + 1) * NODES)
+            nc.scalar.copy(out=pairs[k][:, 1, :, 1], in_=pages[3][:, cols])
+            grouped = keep.tile([P, NODES, 2, 2], BF16, name="out_grouped%d" % k, align_bytes=64)
+            nc.vector.tensor_copy(out=grouped[:], in_=pairs[k][:].rearrange("p u c v -> p c u v"))
+            if k % 2 == 0:
+                out_codes = keep.tile([P, 2 * NODES], I32, name="out_codes%d" % k, align_bytes=64)
+            half = slice((k % 2) * NODES, (k % 2 + 1) * NODES)
+            nc.vector.quantize_mx(
+                out=out_codes[:, half].bitcast(FP8X4),
+                scales=out_scales[:, cols],
+                in_=grouped[:].rearrange("p c u v -> p (c u v)"),
+            )
+            if k % 2 == 1:
+                nc.sync.dma_start(out=out_words[:, (k - 1) * NODES : (k + 1) * NODES], in_=out_codes[:])
+        for quad in range(4):
+            nc.scalar.dma_start(
+                out=out_2[0, 4 * quad : 4 * quad + 4, :].bitcast(I32),
+                in_=out_scales[32 * quad : 32 * quad + 4, :].bitcast(I32),
+            )

@@ -103,7 +103,7 @@ def tile_list_msg_silu_noneP_kernel(
 
         def prepare_wd(half):
             grouped = keep.tile([P, 2, P, PACK], BF16, name="wd_grouped%d" % half, align_bytes=64)
-            nc.scalar.copy(
+            (nc.scalar.copy if half else nc.vector.tensor_copy)(
                 out=grouped[:].rearrange("p i m j -> p m j i"),
                 in_=wd_raw[:].rearrange("p j (m i) -> p m j i", i=PACK)[:, :, :, 2 * half : 2 * half + 2],
             )
@@ -136,7 +136,7 @@ def tile_list_msg_silu_noneP_kernel(
                             stop=(side == 1),
                         )
                 nc.scalar.activation(act[:, 2 * pair : 2 * pair + 2, :], bank[:], SILU)
-            h_rows = keep.tile([P, PACK, EDGES], BF16, name="h_rows%d" % c, tag="after_h_rows%d" % c)
+            h_rows = keep.tile([P, PACK, EDGES], BF16, name="h_rows%d" % c, tag="after_h_rows%d" % c, align_bytes=64)
             for t in range(PACK):
                 nc.scalar.activation(h_rows[:, t, :], act[:, t, :], COPY, scale=sm_sb[:, t : t + 1])
             h_grouped = keep.tile([P, EDGES, PACK], BF16, name="h_grouped%d" % c, tag=tag, align_bytes=64)
@@ -164,7 +164,7 @@ def tile_list_msg_silu_noneP_kernel(
                     start=True,
                     stop=True,
                 )
-            y_sb = keep.tile([P, len(planes), count], F32, name="y%d_%d" % (planes[0], first), tag=tag)
+            y_sb = keep.tile([P, len(planes), count], F32, name="y%d_%d" % (planes[0], first), tag=tag, align_bytes=64)
             nc.scalar.copy(out=y_sb[:], in_=bank[:])
             for u, i in enumerate(planes):
                 nc.vector.tensor_tensor(
@@ -176,14 +176,14 @@ def tile_list_msg_silu_noneP_kernel(
 
         gather_words(0, 1, "words_first")
         gather_scales(0, 1, "after_first_sums")
-        gather_scales(1, 1, "scales_second")
         gather_words(1, 2, "after_weights")
-        prepare_wd(0)
         hidden(0, "after_first_h")
+        gather_scales(1, 2, "after_first_sums")
+        prepare_wd(0)
         wgo_sb = keep.tile([P, J], F32, name="wgo_sb", tag="words_first", align_bytes=64)
         nc.sync.dma_start(out=wgo_sb[:], in_=wgo)
-        gather_scales(2, 2, "after_first_sums")
         gather_words(3, 1, "after_first_h")
+        gather_scales(3, 1, "after_h_rows0")
         pages[3] = keep.tile([P, T], F32, name="page3", tag="after_gathers", align_bytes=64)
         for quarter in range(4):
             nc.gpsimd.memset(pages[3][:, quarter * 512 : (quarter + 1) * 512], 0.0)
@@ -198,31 +198,41 @@ def tile_list_msg_silu_noneP_kernel(
         messages((3,), 2 * EDGES, 2 * EDGES, "y_one", "y_fourth1")
 
         out_rows = out_0.rearrange("(p i) t -> i p t", i=PACK)
-        pairs = [keep.tile([P, 2, NODES, 2], BF16, name="pairs%d" % k) for k in range(PIECES)]
+        rounded = [keep.tile([P, PACK, NODES], BF16, name="rounded%d" % k) for k in range(PIECES)]
         for i in range(PACK):
             nc.sync.dma_start(out=out_rows[i], in_=pages[i][:])
             if i < PACK - 1:
                 for k in range(PIECES):
-                    nc.scalar.copy(out=pairs[k][:, i // 2, :, i % 2], in_=pages[i][:, k * NODES : (k + 1) * NODES])
+                    nc.scalar.copy(out=rounded[k][:, i, :], in_=pages[i][:, k * NODES : (k + 1) * NODES])
         out_scales = keep.tile([P, T], U8, name="out_scales", align_bytes=64)
         out_words = out_1[0].rearrange("p c i -> p (c i)").bitcast(I32)
+
+        def store_scales(cols, other):
+            for quad in range(4):
+                (other if quad % 2 else nc.sync).dma_start(
+                    out=out_2[0, 4 * quad : 4 * quad + 4, cols].bitcast(I32),
+                    in_=out_scales[32 * quad : 32 * quad + 4, cols].bitcast(I32),
+                )
+
         for k in range(PIECES):
             cols = slice(k * NODES, (k + 1) * NODES)
-            nc.scalar.copy(out=pairs[k][:, 1, :, 1], in_=pages[3][:, cols])
-            grouped = keep.tile([P, NODES, 2, 2], BF16, name="out_grouped%d" % k, align_bytes=64)
-            nc.vector.tensor_copy(out=grouped[:], in_=pairs[k][:].rearrange("p u c v -> p c u v"))
+            copy = nc.scalar.copy if k % 2 else nc.vector.tensor_copy
+            copy(out=rounded[k][:, PACK - 1, :], in_=pages[PACK - 1][:, cols])
+            grouped = keep.tile([P, NODES, PACK], BF16, name="out_grouped%d" % k, align_bytes=64)
+            copy(
+                out=grouped[:].rearrange("p (e f) t -> p e t f", f=4),
+                in_=rounded[k][:].rearrange("p t (e f) -> p e t f", f=4),
+            )
             if k % 2 == 0:
                 out_codes = keep.tile([P, 2 * NODES], I32, name="out_codes%d" % k, align_bytes=64)
             half = slice((k % 2) * NODES, (k % 2 + 1) * NODES)
             nc.vector.quantize_mx(
                 out=out_codes[:, half].bitcast(FP8X4),
                 scales=out_scales[:, cols],
-                in_=grouped[:].rearrange("p c u v -> p (c u v)"),
+                in_=grouped[:].rearrange("p c t -> p (c t)"),
             )
             if k % 2 == 1:
                 nc.sync.dma_start(out=out_words[:, (k - 1) * NODES : (k + 1) * NODES], in_=out_codes[:])
-        for quad in range(4):
-            nc.scalar.dma_start(
-                out=out_2[0, 4 * quad : 4 * quad + 4, :].bitcast(I32),
-                in_=out_scales[32 * quad : 32 * quad + 4, :].bitcast(I32),
-            )
+            if k == PIECES - 3:
+                store_scales(slice(0, (k + 1) * NODES), nc.sync)
+        store_scales(slice((PIECES - 2) * NODES, T), nc.scalar)

@@ -44,28 +44,28 @@ def tile_list_msg_silu_noneP_kernel(
         def words_of(packed):
             return packed[0].rearrange("p c i -> p (c i)").bitcast(I32)
 
-        tab_plane = keep.tile([P, T], U8, name="tab_plane", align_bytes=64)
+        tab_plane = keep.tile([P, T], U8, name="tab_plane", tag="after_gathers3", align_bytes=64)
         w_plane = keep.tile([P, R], U8, name="w_plane", tag="after_weights", align_bytes=64)
-        nc.vector.memset(w_plane[:].bitcast(I32), 0)
         nc.vector.memset(tab_plane[:].bitcast(I32), 0)
+        nc.vector.memset(w_plane[:].bitcast(I32), 0)
 
         src_list = keep.tile([P, J // 16], U16, name="src_list")
         dst_list = keep.tile([P, J // 16], U16, name="dst_list")
         sm_sb = keep.tile([P, PACK], F32, name="sm_sb")
         nc.sync.dma_start(src_list[:], offs)
-        tab_sb = keep.tile([P, T], I32, name="tab_sb", tag="after_gathers", align_bytes=64)
+        nc.sync.dma_start(dst_list[:], offs2)
+        tab_sb = keep.tile([P, T], I32, name="tab_sb", tag="after_gathers2", align_bytes=64)
         nc.sync.dma_start(out=tab_sb[:], in_=words_of(tab_words))
         w_raw = keep.tile([P, 2, R], I32, name="w_raw", tag="after_words")
         nc.sync.dma_start(out=w_raw[:, 0, :], in_=words_of(ws_words))
         nc.sync.dma_start(out=w_raw[:, 1, :], in_=words_of(wt_words))
-        nc.sync.dma_start(dst_list[:], offs2)
         load_scale_rows(nc.sync, tab_plane, 0, tab_scales)
         load_scale_rows(nc.sync, w_plane, 0, ws_scales)
-        load_scale_rows(nc.gpsimd, w_plane, 4, wt_scales)
+        load_scale_rows(nc.sync, w_plane, 4, wt_scales)
         nc.gpsimd.dma_start(out=sm_sb[:], in_=sm.rearrange("(p t) -> p t", t=PACK))
 
         pages = {}
-        for i in (0, 1, 2):
+        for i in (0, 1):
             pages[i] = keep.tile([P, T], F32, name="page%d" % i)
             nc.vector.memset(pages[i][:].bitcast(I32), 0)
 
@@ -176,25 +176,27 @@ def tile_list_msg_silu_noneP_kernel(
 
         gather_words(0, 1, "words_first")
         gather_scales(0, 1, "after_first_sums")
+        gather_scales(1, 1, "scales_second")
         gather_words(1, 2, "after_weights")
         hidden(0, "after_first_h")
-        gather_scales(1, 2, "after_first_sums")
+        gather_scales(2, 1, "after_first_sums")
         prepare_wd(0)
         wgo_sb = keep.tile([P, J], F32, name="wgo_sb", tag="words_first", align_bytes=64)
         nc.sync.dma_start(out=wgo_sb[:], in_=wgo)
         gather_words(3, 1, "after_first_h")
         gather_scales(3, 1, "after_h_rows0")
-        pages[3] = keep.tile([P, T], F32, name="page3", tag="after_gathers", align_bytes=64)
-        for quarter in range(4):
-            nc.gpsimd.memset(pages[3][:, quarter * 512 : (quarter + 1) * 512], 0.0)
+        for i in (2, 3):
+            pages[i] = keep.tile([P, T], F32, name="page%d" % i, tag="after_gathers%d" % i, align_bytes=64)
+            for quarter in range(4):
+                nc.gpsimd.memset(pages[i][:, quarter * 512 : (quarter + 1) * 512], 0.0)
         messages((0, 1), 0, EDGES, "y_pair", "y_pair0")
         prepare_wd(1)
         for c in range(1, CHUNKS):
             hidden(c, "h_grouped%d" % c)
-            messages((2,), (c - 1) * EDGES, EDGES, "y_one", "after_h_rows%d" % c)
+            messages((2, 3) if c == 2 else (2,), (c - 1) * EDGES, EDGES, "y_one", "after_h_rows%d" % c)
             messages((0, 1), c * EDGES, EDGES, "y_pair", "y_pair%d" % c)
         messages((2,), (CHUNKS - 1) * EDGES, EDGES, "y_one", "y_third_last")
-        messages((3,), 0, 2 * EDGES, "y_one", "y_fourth0")
+        messages((3,), 0, EDGES, "y_one", "y_fourth0")
         messages((3,), 2 * EDGES, 2 * EDGES, "y_one", "y_fourth1")
 
         out_rows = out_0.rearrange("(p i) t -> i p t", i=PACK)

@@ -23,6 +23,7 @@ CHUNKS = J // EDGES
 LIST_COLS = EDGES // 16
 NODES = 256
 PIECES = T // NODES
+BANK = 512
 
 
 def tile_list_msg_silu_noneP_kernel(
@@ -44,7 +45,7 @@ def tile_list_msg_silu_noneP_kernel(
         def words_of(packed):
             return packed[0].rearrange("p c i -> p (c i)").bitcast(I32)
 
-        tab_plane = keep.tile([P, T], U8, name="tab_plane", tag="after_gathers3", align_bytes=64)
+        tab_plane = keep.tile([P, T], U8, name="tab_plane", align_bytes=64)
         w_plane = keep.tile([P, R], U8, name="w_plane", tag="after_weights", align_bytes=64)
         nc.vector.memset(tab_plane[:].bitcast(I32), 0)
         nc.vector.memset(w_plane[:].bitcast(I32), 0)
@@ -54,7 +55,7 @@ def tile_list_msg_silu_noneP_kernel(
         sm_sb = keep.tile([P, PACK], F32, name="sm_sb")
         nc.sync.dma_start(src_list[:], offs)
         nc.sync.dma_start(dst_list[:], offs2)
-        tab_sb = keep.tile([P, T], I32, name="tab_sb", tag="after_gathers2", align_bytes=64)
+        tab_sb = keep.tile([P, T], I32, name="tab_sb", align_bytes=64)
         nc.sync.dma_start(out=tab_sb[:], in_=words_of(tab_words))
         w_raw = keep.tile([P, 2, R], I32, name="w_raw", tag="after_words")
         nc.sync.dma_start(out=w_raw[:, 0, :], in_=words_of(ws_words))
@@ -65,7 +66,7 @@ def tile_list_msg_silu_noneP_kernel(
         nc.gpsimd.dma_start(out=sm_sb[:], in_=sm.rearrange("(p t) -> p t", t=PACK))
 
         pages = {}
-        for i in (0, 1):
+        for i in (0, 1, 2):
             pages[i] = keep.tile([P, T], F32, name="page%d" % i)
             nc.vector.memset(pages[i][:].bitcast(I32), 0)
 
@@ -84,20 +85,20 @@ def tile_list_msg_silu_noneP_kernel(
         lists = (src_list, dst_list)
         picked_words, picked_scales = {}, {}
 
-        def gather(window, dtype, picked, first, count, tag):
-            got = keep.tile([P, 2, count * EDGES], dtype, name="%s_%d" % (tag, first), tag=tag, align_bytes=64)
-            for side in (0, 1):
+        def gather(window, dtype, picked, first, count, tag, sides):
+            got = keep.tile([P, len(sides), count * EDGES], dtype, name="%s_%d" % (tag, first), tag=tag, align_bytes=64)
+            for u, side in enumerate(sides):
                 nc.vector.tensor_copy(
-                    got[:, side, :], window.indirect(lists[side][:, first * LIST_COLS : (first + count) * LIST_COLS])
+                    got[:, u, :], window.indirect(lists[side][:, first * LIST_COLS : (first + count) * LIST_COLS])
                 )
                 for c in range(count):
-                    picked[first + c, side] = got[:, side, c * EDGES : (c + 1) * EDGES]
+                    picked[first + c, side] = got[:, u, c * EDGES : (c + 1) * EDGES]
 
-        def gather_words(first, count, tag):
-            gather(tab_sb[:].bitcast(U32), U32, picked_words, first, count, tag)
+        def gather_words(first, count, tag, sides=(0, 1)):
+            gather(tab_sb[:].bitcast(U32), U32, picked_words, first, count, tag, sides)
 
         def gather_scales(first, count, tag):
-            gather(tab_plane[:], U8, picked_scales, first, count, tag)
+            gather(tab_plane[:], U8, picked_scales, first, count, tag, (0, 1))
 
         wd_codes, wd_scales = {}, {}
 
@@ -152,89 +153,97 @@ def tile_list_msg_silu_noneP_kernel(
             )
 
         def messages(planes, first, count, bank_name, tag):
-            cols = slice(first, first + count)
-            bank = psum.tile([P, len(planes), count], F32, name=bank_name)
-            for u, i in enumerate(planes):
-                nc.tensor.matmul_mx(
-                    out=bank[:, u, :],
-                    lhsT=wd_codes[i].bitcast(FP8X4),
-                    lhsT_scale=wd_scales[i],
-                    rhs=h_codes[:, cols].bitcast(FP8X4),
-                    rhs_scale=h_scales[:, cols],
-                    start=True,
-                    stop=True,
-                )
             y_sb = keep.tile([P, len(planes), count], F32, name="y%d_%d" % (planes[0], first), tag=tag, align_bytes=64)
-            nc.scalar.copy(out=y_sb[:], in_=bank[:])
+            width = min(count, BANK // len(planes))
+            for start in range(0, count, width):
+                cols = slice(first + start, first + start + width)
+                bank = psum.tile([P, len(planes), width], F32, name=bank_name)
+                for u, i in enumerate(planes):
+                    nc.tensor.matmul_mx(
+                        out=bank[:, u, :],
+                        lhsT=wd_codes[i].bitcast(FP8X4),
+                        lhsT_scale=wd_scales[i],
+                        rhs=h_codes[:, cols].bitcast(FP8X4),
+                        rhs_scale=h_scales[:, cols],
+                        start=True,
+                        stop=True,
+                    )
+                nc.scalar.copy(out=y_sb[:, :, start : start + width], in_=bank[:])
             for u, i in enumerate(planes):
                 nc.vector.tensor_tensor(
                     pages[i][:].indirect(dst_list[:, first // 16 : (first + count) // 16]),
                     y_sb[:, u, :],
-                    wgo_sb[:, cols],
+                    wgo_sb[:, first : first + count],
                     MULT,
                 )
 
-        gather_words(0, 1, "words_first")
+        gather_words(0, 1, "words_first", (0,))
+        gather_words(0, 1, "words_first_dst", (1,))
         gather_scales(0, 1, "after_first_sums")
         gather_scales(1, 1, "scales_second")
         gather_words(1, 2, "after_weights")
+        prepare_wd(1)
         hidden(0, "after_first_h")
         gather_scales(2, 1, "after_first_sums")
+        pages[3] = keep.tile([P, T], F32, name="page3", tag="words_first_dst", align_bytes=64)
+        nc.vector.memset(pages[3][:].bitcast(I32), 0)
         prepare_wd(0)
         wgo_sb = keep.tile([P, J], F32, name="wgo_sb", tag="words_first", align_bytes=64)
         nc.sync.dma_start(out=wgo_sb[:], in_=wgo)
         gather_words(3, 1, "after_first_h")
         gather_scales(3, 1, "after_h_rows0")
-        for i in (2, 3):
-            pages[i] = keep.tile([P, T], F32, name="page%d" % i, tag="after_gathers%d" % i, align_bytes=64)
-            for quarter in range(4):
-                nc.gpsimd.memset(pages[i][:, quarter * 512 : (quarter + 1) * 512], 0.0)
         messages((0, 1), 0, EDGES, "y_pair", "y_pair0")
-        prepare_wd(1)
         for c in range(1, CHUNKS):
             hidden(c, "h_grouped%d" % c)
-            messages((2, 3) if c == 2 else (2,), (c - 1) * EDGES, EDGES, "y_one", "after_h_rows%d" % c)
+            messages((2,), (c - 1) * EDGES, EDGES, "y_one", "after_h_rows%d" % c)
             messages((0, 1), c * EDGES, EDGES, "y_pair", "y_pair%d" % c)
         messages((2,), (CHUNKS - 1) * EDGES, EDGES, "y_one", "y_third_last")
-        messages((3,), 0, EDGES, "y_one", "y_fourth0")
-        messages((3,), 2 * EDGES, 2 * EDGES, "y_one", "y_fourth1")
+        messages((3,), 0, J, "y_one", "y_fourth")
 
         out_rows = out_0.rearrange("(p i) t -> i p t", i=PACK)
-        rounded = [keep.tile([P, PACK, NODES], BF16, name="rounded%d" % k) for k in range(PIECES)]
+        by_rows = {0: nc.vector.tensor_copy, PIECES - 1: nc.scalar.copy}
+        slots = []
+        for k in range(PIECES):
+            if k in by_rows:
+                rows = keep.tile([P, PACK, NODES], BF16, name="rows%d" % k)
+                slots.append((rows, [rows[:, i, :] for i in range(PACK)]))
+            else:
+                pairs = keep.tile([P, 2, NODES, 2], BF16, name="pairs%d" % k)
+                slots.append((pairs, [pairs[:, i // 2, :, i % 2] for i in range(PACK)]))
         for i in range(PACK):
             nc.sync.dma_start(out=out_rows[i], in_=pages[i][:])
             if i < PACK - 1:
                 for k in range(PIECES):
-                    nc.scalar.copy(out=rounded[k][:, i, :], in_=pages[i][:, k * NODES : (k + 1) * NODES])
-        out_scales = keep.tile([P, T], U8, name="out_scales", align_bytes=64)
+                    nc.scalar.copy(out=slots[k][1][i], in_=pages[i][:, k * NODES : (k + 1) * NODES])
+        out_scales = keep.tile([P, 2 * NODES], U8, name="out_scales", align_bytes=64)
         out_words = out_1[0].rearrange("p c i -> p (c i)").bitcast(I32)
-
-        def store_scales(cols, other):
-            for quad in range(4):
-                (other if quad % 2 else nc.sync).dma_start(
-                    out=out_2[0, 4 * quad : 4 * quad + 4, cols].bitcast(I32),
-                    in_=out_scales[32 * quad : 32 * quad + 4, cols].bitcast(I32),
-                )
 
         for k in range(PIECES):
             cols = slice(k * NODES, (k + 1) * NODES)
-            copy = nc.scalar.copy if k % 2 else nc.vector.tensor_copy
-            copy(out=rounded[k][:, PACK - 1, :], in_=pages[PACK - 1][:, cols])
+            staged, places = slots[k]
             grouped = keep.tile([P, NODES, PACK], BF16, name="out_grouped%d" % k, align_bytes=64)
-            copy(
-                out=grouped[:].rearrange("p (e f) t -> p e t f", f=4),
-                in_=rounded[k][:].rearrange("p t (e f) -> p e t f", f=4),
-            )
+            by_rows.get(k, nc.scalar.copy)(out=places[PACK - 1], in_=pages[PACK - 1][:, cols])
+            if k in by_rows:
+                by_rows[k](
+                    out=grouped[:].rearrange("p (e f) t -> p e t f", f=4),
+                    in_=staged[:].rearrange("p t (e f) -> p e t f", f=4),
+                )
+            else:
+                nc.vector.tensor_copy(
+                    out=grouped[:].rearrange("p c (u v) -> p c u v", v=2), in_=staged[:].rearrange("p u c v -> p c u v")
+                )
             if k % 2 == 0:
                 out_codes = keep.tile([P, 2 * NODES], I32, name="out_codes%d" % k, align_bytes=64)
             half = slice((k % 2) * NODES, (k % 2 + 1) * NODES)
             nc.vector.quantize_mx(
                 out=out_codes[:, half].bitcast(FP8X4),
-                scales=out_scales[:, cols],
+                scales=out_scales[4 * (k // 2) :, half],
                 in_=grouped[:].rearrange("p c t -> p (c t)"),
             )
             if k % 2 == 1:
                 nc.sync.dma_start(out=out_words[:, (k - 1) * NODES : (k + 1) * NODES], in_=out_codes[:])
-            if k == PIECES - 3:
-                store_scales(slice(0, (k + 1) * NODES), nc.sync)
-        store_scales(slice((PIECES - 2) * NODES, T), nc.scalar)
+        for quad in range(4):
+            (nc.scalar if quad % 2 else nc.sync).dma_start(
+                out=out_2[0, 4 * quad : 4 * quad + 4, :].bitcast(I32).rearrange("r (g c) -> g r c", g=4),
+                in_=out_scales[32 * quad : 32 * quad + 16, :].bitcast(I32),
+            )

@@ -32,7 +32,6 @@ def tile_list_msg_silu_noneP_kernel(
     nc = tc.nc
     with ExitStack() as ctx:
         keep = ctx.enter_context(tc.tile_pool(name="keep", bufs=1))
-        ring = ctx.enter_context(tc.tile_pool(name="ring", bufs=2))
         psum = ctx.enter_context(tc.psum_pool(name="psum", bufs=2))
 
         def load_scale_rows(queue, plane, first, rows):
@@ -66,22 +65,12 @@ def tile_list_msg_silu_noneP_kernel(
         nc.gpsimd.dma_start(out=sm_sb[:], in_=sm.rearrange("(p t) -> p t", t=PACK))
 
         pages = {}
-        for i in (0, 1, 2):
+        for i in range(PACK):
             pages[i] = keep.tile([P, T], F32, name="page%d" % i)
             nc.vector.memset(pages[i][:].bitcast(I32), 0)
 
         w_codes = keep.tile([P, 2, PACK, P], I32, name="w_codes", align_bytes=64)
         w_scales = keep.tile([P, PACK, P], U8, name="w_scales", align_bytes=64)
-        nc.vector.tensor_copy(
-            out=w_codes[:].rearrange("p w t m -> p w m t"), in_=w_raw[:].rearrange("p w (m t) -> p w m t", t=PACK)
-        )
-        nc.vector.tensor_copy(
-            out=w_scales[:].rearrange("p t m -> p m t"), in_=w_plane[:].rearrange("p (m t) -> p m t", t=PACK)
-        )
-
-        wd_raw = keep.tile([P, PACK, N], F32, name="wd_raw", tag="after_words")
-        nc.sync.dma_start(out=wd_raw[:], in_=wd.rearrange("(p j) n -> p j n", j=PACK))
-
         lists = (src_list, dst_list)
         picked_words, picked_scales = {}, {}
 
@@ -100,28 +89,25 @@ def tile_list_msg_silu_noneP_kernel(
         def gather_scales(first, count, tag):
             gather(tab_plane[:], U8, picked_scales, first, count, tag, (0, 1))
 
-        wd_codes, wd_scales = {}, {}
+        wd_codes = keep.tile([P, PACK, P], U32, name="wd_codes", align_bytes=64)
+        wd_scales = keep.tile([P, PACK, P], U8, name="wd_scales", align_bytes=64)
 
-        def prepare_wd(half):
-            grouped = keep.tile([P, 2, P, PACK], BF16, name="wd_grouped%d" % half, align_bytes=64)
-            (nc.scalar.copy if half else nc.vector.tensor_copy)(
-                out=grouped[:].rearrange("p i m j -> p m j i"),
-                in_=wd_raw[:].rearrange("p j (m i) -> p m j i", i=PACK)[:, :, :, 2 * half : 2 * half + 2],
+        def prepare_wd():
+            grouped = keep.tile([P, PACK, P, PACK], BF16, name="wd_grouped", align_bytes=64)
+            nc.vector.tensor_copy(
+                out=grouped[:].rearrange("p i m j -> p m j i"), in_=wd_raw[:].rearrange("p j (m i) -> p m j i", i=PACK)
             )
-            codes = keep.tile([P, 2 * P], U32, name="wd_codes%d" % half, align_bytes=64)
-            scales = keep.tile([P, 2 * P], U8, name="wd_scales%d" % half, align_bytes=64)
             nc.vector.quantize_mx(
-                out=codes[:].bitcast(FP8X4), scales=scales[:], in_=grouped[:].rearrange("p i m j -> p (i m j)")
+                out=wd_codes[:].rearrange("p i m -> p (i m)").bitcast(FP8X4),
+                scales=wd_scales[:].rearrange("p i m -> p (i m)"),
+                in_=grouped[:].rearrange("p i m j -> p (i m j)"),
             )
-            for i in (0, 1):
-                wd_codes[2 * half + i] = codes[:, i * P : (i + 1) * P]
-                wd_scales[2 * half + i] = scales[:, i * P : (i + 1) * P]
 
         h_codes = keep.tile([P, J], U32, name="h_codes", align_bytes=64)
         h_scales = keep.tile([P, J], U8, name="h_scales", align_bytes=64)
 
         def hidden(c, tag):
-            act = ring.tile([P, PACK, EDGES], F32, name="act")
+            act = keep.tile([P, PACK, EDGES], F32, name="act")
             for pair in (0, 1):
                 bank = psum.tile([P, 2, EDGES], F32, name="a_bank%d" % pair)
                 for u in (0, 1):
@@ -161,8 +147,8 @@ def tile_list_msg_silu_noneP_kernel(
                 for u, i in enumerate(planes):
                     nc.tensor.matmul_mx(
                         out=bank[:, u, :],
-                        lhsT=wd_codes[i].bitcast(FP8X4),
-                        lhsT_scale=wd_scales[i],
+                        lhsT=wd_codes[:, i, :].bitcast(FP8X4),
+                        lhsT_scale=wd_scales[:, i, :],
                         rhs=h_codes[:, cols].bitcast(FP8X4),
                         rhs_scale=h_scales[:, cols],
                         start=True,
@@ -177,17 +163,20 @@ def tile_list_msg_silu_noneP_kernel(
                     MULT,
                 )
 
-        gather_words(0, 1, "words_first", (0,))
-        gather_words(0, 1, "words_first_dst", (1,))
+        gather_words(0, 1, "words_first")
+        nc.vector.tensor_copy(
+            out=w_codes[:].rearrange("p w t m -> p w m t"), in_=w_raw[:].rearrange("p w (m t) -> p w m t", t=PACK)
+        )
+        wd_raw = keep.tile([P, PACK, N], F32, name="wd_raw", tag="after_words")
+        nc.sync.dma_start(out=wd_raw[:], in_=wd.rearrange("(p j) n -> p j n", j=PACK))
         gather_scales(0, 1, "after_first_sums")
-        gather_scales(1, 1, "scales_second")
+        nc.vector.tensor_copy(
+            out=w_scales[:].rearrange("p t m -> p m t"), in_=w_plane[:].rearrange("p (m t) -> p m t", t=PACK)
+        )
         gather_words(1, 2, "after_weights")
-        prepare_wd(1)
         hidden(0, "after_first_h")
-        gather_scales(2, 1, "after_first_sums")
-        pages[3] = keep.tile([P, T], F32, name="page3", tag="words_first_dst", align_bytes=64)
-        nc.vector.memset(pages[3][:].bitcast(I32), 0)
-        prepare_wd(0)
+        gather_scales(1, 2, "after_first_sums")
+        prepare_wd()
         wgo_sb = keep.tile([P, J], F32, name="wgo_sb", tag="words_first", align_bytes=64)
         nc.sync.dma_start(out=wgo_sb[:], in_=wgo)
         gather_words(3, 1, "after_first_h")
@@ -240,7 +229,9 @@ def tile_list_msg_silu_noneP_kernel(
                 scales=out_scales[4 * (k // 2) :, half],
                 in_=grouped[:].rearrange("p c t -> p (c t)"),
             )
-            if k % 2 == 1:
+            if k >= PIECES - 2:
+                nc.sync.dma_start(out=out_words[:, cols], in_=out_codes[:, half])
+            elif k % 2 == 1:
                 nc.sync.dma_start(out=out_words[:, (k - 1) * NODES : (k + 1) * NODES], in_=out_codes[:])
         for quad in range(4):
             (nc.scalar if quad % 2 else nc.sync).dma_start(

@@ -21,8 +21,12 @@ PACK = 4
 EDGES = 256
 CHUNKS = J // EDGES
 LIST_COLS = EDGES // 16
-NODES = 256
-PIECES = T // NODES
+GROUP = 512
+CLOSING = (
+    [(128, "rows"), (128, "pairs")]
+    + [(256, "pairs")] * 5
+    + [(128, "pairs"), (256, "pairs on Scalar"), (128, "pairs on Scalar")]
+)
 BANK = 512
 
 
@@ -46,20 +50,26 @@ def tile_list_msg_silu_noneP_kernel(
 
         tab_plane = keep.tile([P, T], U8, name="tab_plane", align_bytes=64)
         w_plane = keep.tile([P, R], U8, name="w_plane", tag="after_weights", align_bytes=64)
-        nc.vector.memset(tab_plane[:].bitcast(I32), 0)
-        nc.vector.memset(w_plane[:].bitcast(I32), 0)
+
+        def clear_on_own_port(words):
+            odd = words.shape[1] // 2 - 1
+            nc.vector.memset(words[:, :odd], 0)
+            nc.vector.memset(words[:, odd:], 0)
+
+        nc.gpsimd.memset(tab_plane[:].bitcast(I32), 0)
+        clear_on_own_port(w_plane[:].bitcast(I32))
 
         src_list = keep.tile([P, J // 16], U16, name="src_list")
         dst_list = keep.tile([P, J // 16], U16, name="dst_list")
         sm_sb = keep.tile([P, PACK], F32, name="sm_sb")
         nc.sync.dma_start(src_list[:], offs)
         nc.sync.dma_start(dst_list[:], offs2)
+        load_scale_rows(nc.sync, tab_plane, 0, tab_scales)
         tab_sb = keep.tile([P, T], I32, name="tab_sb", align_bytes=64)
         nc.sync.dma_start(out=tab_sb[:], in_=words_of(tab_words))
         w_raw = keep.tile([P, 2, R], I32, name="w_raw", tag="after_words")
         nc.sync.dma_start(out=w_raw[:, 0, :], in_=words_of(ws_words))
         nc.sync.dma_start(out=w_raw[:, 1, :], in_=words_of(wt_words))
-        load_scale_rows(nc.sync, tab_plane, 0, tab_scales)
         load_scale_rows(nc.sync, w_plane, 0, ws_scales)
         load_scale_rows(nc.sync, w_plane, 4, wt_scales)
         nc.gpsimd.dma_start(out=sm_sb[:], in_=sm.rearrange("(p t) -> p t", t=PACK))
@@ -67,7 +77,10 @@ def tile_list_msg_silu_noneP_kernel(
         pages = {}
         for i in range(PACK):
             pages[i] = keep.tile([P, T], F32, name="page%d" % i)
-            nc.vector.memset(pages[i][:].bitcast(I32), 0)
+            if i == 0:
+                clear_on_own_port(pages[i][:].bitcast(I32))
+            else:
+                nc.gpsimd.memset(pages[i][:].bitcast(I32), 0)
 
         w_codes = keep.tile([P, 2, PACK, P], I32, name="w_codes", align_bytes=64)
         w_scales = keep.tile([P, PACK, P], U8, name="w_scales", align_bytes=64)
@@ -163,19 +176,20 @@ def tile_list_msg_silu_noneP_kernel(
                     MULT,
                 )
 
+        gather_scales(0, 1, "after_first_sums")
+        gather_scales(1, 1, "scales_second")
         gather_words(0, 1, "words_first")
         nc.vector.tensor_copy(
             out=w_codes[:].rearrange("p w t m -> p w m t"), in_=w_raw[:].rearrange("p w (m t) -> p w m t", t=PACK)
         )
         wd_raw = keep.tile([P, PACK, N], F32, name="wd_raw", tag="after_words")
         nc.sync.dma_start(out=wd_raw[:], in_=wd.rearrange("(p j) n -> p j n", j=PACK))
-        gather_scales(0, 1, "after_first_sums")
         nc.vector.tensor_copy(
             out=w_scales[:].rearrange("p t m -> p m t"), in_=w_plane[:].rearrange("p (m t) -> p m t", t=PACK)
         )
         gather_words(1, 2, "after_weights")
         hidden(0, "after_first_h")
-        gather_scales(1, 2, "after_first_sums")
+        gather_scales(2, 1, "after_first_sums")
         prepare_wd()
         wgo_sb = keep.tile([P, J], F32, name="wgo_sb", tag="words_first", align_bytes=64)
         nc.sync.dma_start(out=wgo_sb[:], in_=wgo)
@@ -190,49 +204,63 @@ def tile_list_msg_silu_noneP_kernel(
         messages((3,), 0, J, "y_one", "y_fourth")
 
         out_rows = out_0.rearrange("(p i) t -> i p t", i=PACK)
-        by_rows = {0: nc.vector.tensor_copy, PIECES - 1: nc.scalar.copy}
-        slots = []
-        for k in range(PIECES):
-            if k in by_rows:
-                rows = keep.tile([P, PACK, NODES], BF16, name="rows%d" % k)
-                slots.append((rows, [rows[:, i, :] for i in range(PACK)]))
+        pieces = []
+        start = 0
+        for width, kind in CLOSING:
+            cols = slice(start, start + width)
+            if kind == "rows":
+                staged = keep.tile([P, PACK, width], BF16, name="rows%d" % start)
+                places = [staged[:, i, :] for i in range(PACK)]
             else:
-                pairs = keep.tile([P, 2, NODES, 2], BF16, name="pairs%d" % k)
-                slots.append((pairs, [pairs[:, i // 2, :, i % 2] for i in range(PACK)]))
+                staged = keep.tile([P, 2, width, 2], BF16, name="pairs%d" % start)
+                places = [staged[:, i // 2, :, i % 2] for i in range(PACK)]
+            pieces.append((cols, kind, staged, places))
+            start = cols.stop
         for i in range(PACK):
             nc.sync.dma_start(out=out_rows[i], in_=pages[i][:])
             if i < PACK - 1:
-                for k in range(PIECES):
-                    nc.scalar.copy(out=slots[k][1][i], in_=pages[i][:, k * NODES : (k + 1) * NODES])
-        out_scales = keep.tile([P, 2 * NODES], U8, name="out_scales", align_bytes=64)
+                for cols, kind, staged, places in pieces:
+                    nc.scalar.copy(out=places[i], in_=pages[i][:, cols])
+        out_scales = keep.tile([P, GROUP], U8, name="out_scales", align_bytes=64)
         out_words = out_1[0].rearrange("p c i -> p (c i)").bitcast(I32)
+        out_codes = [keep.tile([P, GROUP], I32, name="out_codes%d" % g, align_bytes=64) for g in range(T // GROUP)]
 
-        for k in range(PIECES):
-            cols = slice(k * NODES, (k + 1) * NODES)
-            staged, places = slots[k]
-            grouped = keep.tile([P, NODES, PACK], BF16, name="out_grouped%d" % k, align_bytes=64)
-            by_rows.get(k, nc.scalar.copy)(out=places[PACK - 1], in_=pages[PACK - 1][:, cols])
-            if k in by_rows:
-                by_rows[k](
+        def interleave(cols, kind, staged, places):
+            grouped = keep.tile([P, cols.stop - cols.start, PACK], BF16, name="grouped%d" % cols.start, align_bytes=64)
+            if kind == "rows":
+                nc.vector.tensor_copy(out=places[PACK - 1], in_=pages[PACK - 1][:, cols])
+                nc.vector.tensor_copy(
                     out=grouped[:].rearrange("p (e f) t -> p e t f", f=4),
                     in_=staged[:].rearrange("p t (e f) -> p e t f", f=4),
                 )
             else:
-                nc.vector.tensor_copy(
-                    out=grouped[:].rearrange("p c (u v) -> p c u v", v=2), in_=staged[:].rearrange("p u c v -> p c u v")
+                nc.scalar.copy(out=places[PACK - 1], in_=pages[PACK - 1][:, cols])
+                move, word = (nc.vector.tensor_copy, I32) if kind == "pairs" else (nc.scalar.copy, U32)
+                move(
+                    out=grouped[:].rearrange("p c t -> p (c t)").bitcast(word).rearrange("p (c u) -> p c u", u=2),
+                    in_=staged[:].rearrange("p u c v -> p (u c v)").bitcast(word).rearrange("p (u c) -> p c u", u=2),
                 )
-            if k % 2 == 0:
-                out_codes = keep.tile([P, 2 * NODES], I32, name="out_codes%d" % k, align_bytes=64)
-            half = slice((k % 2) * NODES, (k % 2 + 1) * NODES)
+            return grouped
+
+        def quantise(cols, grouped):
+            g = cols.start // GROUP
+            inside = slice(cols.start - g * GROUP, cols.stop - g * GROUP)
             nc.vector.quantize_mx(
-                out=out_codes[:, half].bitcast(FP8X4),
-                scales=out_scales[4 * (k // 2) :, half],
+                out=out_codes[g][:, inside].bitcast(FP8X4),
+                scales=out_scales[4 * g :, inside],
                 in_=grouped[:].rearrange("p c t -> p (c t)"),
             )
-            if k >= PIECES - 2:
-                nc.sync.dma_start(out=out_words[:, cols], in_=out_codes[:, half])
-            elif k % 2 == 1:
-                nc.sync.dma_start(out=out_words[:, (k - 1) * NODES : (k + 1) * NODES], in_=out_codes[:])
+            if g == T // GROUP - 1:
+                nc.sync.dma_start(out=out_words[:, cols], in_=out_codes[g][:, inside])
+            elif inside.stop == GROUP:
+                nc.sync.dma_start(out=out_words[:, g * GROUP : (g + 1) * GROUP], in_=out_codes[g][:])
+
+        ready = interleave(*pieces[0])
+        for k, piece in enumerate(pieces):
+            done = ready
+            if k + 1 < len(pieces):
+                ready = interleave(*pieces[k + 1])
+            quantise(piece[0], done)
         for quad in range(4):
             (nc.scalar if quad % 2 else nc.sync).dma_start(
                 out=out_2[0, 4 * quad : 4 * quad + 4, :].bitcast(I32).rearrange("r (g c) -> g r c", g=4),

@@ -18,6 +18,7 @@ MULT = mybir.AluOpType.mult
 
 P = 128
 PACK = 4
+RUN = 8
 EDGES = 256
 CHUNKS = J // EDGES
 LIST_COLS = EDGES // 16
@@ -50,18 +51,11 @@ def tile_list_msg_silu_noneP_kernel(
 
         tab_plane = keep.tile([P, T], U8, name="tab_plane", align_bytes=64)
         w_plane = keep.tile([P, R], U8, name="w_plane", tag="after_weights", align_bytes=64)
-
-        def clear_on_own_port(words):
-            odd = words.shape[1] // 2 - 1
-            nc.vector.memset(words[:, :odd], 0)
-            nc.vector.memset(words[:, odd:], 0)
-
         nc.gpsimd.memset(tab_plane[:].bitcast(I32), 0)
-        clear_on_own_port(w_plane[:].bitcast(I32))
+        nc.gpsimd.memset(w_plane[:].bitcast(I32), 0)
 
         src_list = keep.tile([P, J // 16], U16, name="src_list")
         dst_list = keep.tile([P, J // 16], U16, name="dst_list")
-        sm_sb = keep.tile([P, PACK], F32, name="sm_sb")
         nc.sync.dma_start(src_list[:], offs)
         nc.sync.dma_start(dst_list[:], offs2)
         load_scale_rows(nc.sync, tab_plane, 0, tab_scales)
@@ -72,15 +66,18 @@ def tile_list_msg_silu_noneP_kernel(
         nc.sync.dma_start(out=w_raw[:, 1, :], in_=words_of(wt_words))
         load_scale_rows(nc.sync, w_plane, 0, ws_scales)
         load_scale_rows(nc.sync, w_plane, 4, wt_scales)
-        nc.gpsimd.dma_start(out=sm_sb[:], in_=sm.rearrange("(p t) -> p t", t=PACK))
+        sm_sb = keep.tile([P, PACK, RUN], F32, name="sm_sb")
+        sm_cols = [sm_sb[:, t, 0:1] for t in range(PACK)]
+        with nc.allow_non_contiguous_dma(reason="one factor for each partition"):
+            for t in range(PACK):
+                nc.sync.dma_start(out=sm_cols[t], in_=sm.rearrange("(b t c o) -> t b c o", t=PACK, c=RUN, o=1)[t])
 
         pages = {}
         for i in range(PACK):
             pages[i] = keep.tile([P, T], F32, name="page%d" % i)
-            if i == 0:
-                clear_on_own_port(pages[i][:].bitcast(I32))
-            else:
-                nc.gpsimd.memset(pages[i][:].bitcast(I32), 0)
+            width = GROUP if i == 0 else T
+            for start in range(0, T, width):
+                nc.vector.memset(pages[i][:, start : start + width].bitcast(I32), 0)
 
         w_codes = keep.tile([P, 2, PACK, P], I32, name="w_codes", align_bytes=64)
         w_scales = keep.tile([P, PACK, P], U8, name="w_scales", align_bytes=64)
@@ -138,7 +135,7 @@ def tile_list_msg_silu_noneP_kernel(
                 nc.scalar.activation(act[:, 2 * pair : 2 * pair + 2, :], bank[:], SILU)
             h_rows = keep.tile([P, PACK, EDGES], BF16, name="h_rows%d" % c, tag="after_h_rows%d" % c, align_bytes=64)
             for t in range(PACK):
-                nc.scalar.activation(h_rows[:, t, :], act[:, t, :], COPY, scale=sm_sb[:, t : t + 1])
+                nc.scalar.activation(h_rows[:, t, :], act[:, t, :], COPY, scale=sm_cols[t])
             h_grouped = keep.tile([P, EDGES, PACK], BF16, name="h_grouped%d" % c, tag=tag, align_bytes=64)
             nc.scalar.copy(
                 out=h_grouped[:].rearrange("p (e f) t -> p e t f", f=4),
@@ -180,12 +177,15 @@ def tile_list_msg_silu_noneP_kernel(
         gather_scales(1, 1, "scales_second")
         gather_words(0, 1, "words_first")
         nc.vector.tensor_copy(
-            out=w_codes[:].rearrange("p w t m -> p w m t"), in_=w_raw[:].rearrange("p w (m t) -> p w m t", t=PACK)
+            out=w_codes[:].rearrange("p w t (b c) -> p w t b c", c=RUN),
+            in_=w_raw[:].rearrange("p w (b t c) -> p w t b c", t=PACK, c=RUN),
         )
         wd_raw = keep.tile([P, PACK, N], F32, name="wd_raw", tag="after_words")
-        nc.sync.dma_start(out=wd_raw[:], in_=wd.rearrange("(p j) n -> p j n", j=PACK))
+        for t in range(PACK):
+            nc.sync.dma_start(out=wd_raw[:, t, :], in_=wd.rearrange("(b t c) n -> t b c n", t=PACK, c=RUN)[t])
         nc.vector.tensor_copy(
-            out=w_scales[:].rearrange("p t m -> p m t"), in_=w_plane[:].rearrange("p (m t) -> p m t", t=PACK)
+            out=w_scales[:].rearrange("p t m -> p (t m)").bitcast(I32).rearrange("p (t b c) -> p t b c", t=PACK, c=RUN // 4),
+            in_=w_plane[:].bitcast(I32).rearrange("p (b t c) -> p t b c", t=PACK, c=RUN // 4),
         )
         gather_words(1, 2, "after_weights")
         hidden(0, "after_first_h")

@@ -39,9 +39,9 @@ def tile_list_msg_silu_noneP_kernel(
         keep = ctx.enter_context(tc.tile_pool(name="keep", bufs=1))
         psum = ctx.enter_context(tc.psum_pool(name="psum", bufs=2))
 
-        def load_scale_rows(queue, plane, first, rows):
-            for quad in range(4):
-                queue.dma_start(
+        def load_scale_rows(plane, first, rows, quads):
+            for quad in quads:
+                nc.sync.dma_start(
                     out=plane[32 * quad + first : 32 * quad + first + 4, :].bitcast(I32),
                     in_=rows[0, 4 * quad : 4 * quad + 4, :].bitcast(I32),
                 )
@@ -51,33 +51,37 @@ def tile_list_msg_silu_noneP_kernel(
 
         tab_plane = keep.tile([P, T], U8, name="tab_plane", align_bytes=64)
         w_plane = keep.tile([P, R], U8, name="w_plane", tag="after_weights", align_bytes=64)
-        nc.gpsimd.memset(tab_plane[:].bitcast(I32), 0)
-        nc.gpsimd.memset(w_plane[:].bitcast(I32), 0)
+        nc.vector.memset(tab_plane[:].bitcast(I32), 0)
+        nc.vector.memset(w_plane[:].bitcast(I32), 0)
 
         src_list = keep.tile([P, J // 16], U16, name="src_list")
         dst_list = keep.tile([P, J // 16], U16, name="dst_list")
         nc.sync.dma_start(src_list[:], offs)
         nc.sync.dma_start(dst_list[:], offs2)
-        load_scale_rows(nc.sync, tab_plane, 0, tab_scales)
-        tab_sb = keep.tile([P, T], I32, name="tab_sb", align_bytes=64)
-        nc.sync.dma_start(out=tab_sb[:], in_=words_of(tab_words))
-        w_raw = keep.tile([P, 2, R], I32, name="w_raw", tag="after_words")
+        load_scale_rows(tab_plane, 0, tab_scales, range(4))
+        w_raw = keep.tile([P, 2, R], I32, name="w_raw")
         nc.sync.dma_start(out=w_raw[:, 0, :], in_=words_of(ws_words))
         nc.sync.dma_start(out=w_raw[:, 1, :], in_=words_of(wt_words))
-        load_scale_rows(nc.sync, w_plane, 0, ws_scales)
-        load_scale_rows(nc.sync, w_plane, 4, wt_scales)
+        load_scale_rows(w_plane, 0, ws_scales, range(1))
+        tab_sb = keep.tile([P, T], I32, name="tab_sb", align_bytes=64)
+        nc.sync.dma_start(out=tab_sb[:], in_=words_of(tab_words))
+        load_scale_rows(w_plane, 0, ws_scales, range(1, 4))
+        load_scale_rows(w_plane, 4, wt_scales, range(4))
         sm_sb = keep.tile([P, PACK, RUN], F32, name="sm_sb")
         sm_cols = [sm_sb[:, t, 0:1] for t in range(PACK)]
         with nc.allow_non_contiguous_dma(reason="one factor for each partition"):
             for t in range(PACK):
                 nc.sync.dma_start(out=sm_cols[t], in_=sm.rearrange("(b t c o) -> t b c o", t=PACK, c=RUN, o=1)[t])
+        wd_raw = keep.tile([P, PACK, N], F32, name="wd_raw")
+        for t in range(PACK):
+            nc.sync.dma_start(out=wd_raw[:, t, :], in_=wd.rearrange("(b t c) n -> t b c n", t=PACK, c=RUN)[t])
+        wgo_sb = keep.tile([P, J], F32, name="wgo_sb", align_bytes=64)
+        nc.sync.dma_start(out=wgo_sb[:], in_=wgo)
 
         pages = {}
         for i in range(PACK):
             pages[i] = keep.tile([P, T], F32, name="page%d" % i)
-            width = GROUP if i == 0 else T
-            for start in range(0, T, width):
-                nc.vector.memset(pages[i][:, start : start + width].bitcast(I32), 0)
+            nc.vector.memset(pages[i][:].bitcast(I32), 0)
 
         w_codes = keep.tile([P, 2, PACK, P], I32, name="w_codes", align_bytes=64)
         w_scales = keep.tile([P, PACK, P], U8, name="w_scales", align_bytes=64)
@@ -96,8 +100,8 @@ def tile_list_msg_silu_noneP_kernel(
         def gather_words(first, count, tag, sides=(0, 1)):
             gather(tab_sb[:].bitcast(U32), U32, picked_words, first, count, tag, sides)
 
-        def gather_scales(first, count, tag):
-            gather(tab_plane[:], U8, picked_scales, first, count, tag, (0, 1))
+        def gather_scales(first, count, tag, sides=(0, 1)):
+            gather(tab_plane[:], U8, picked_scales, first, count, tag, sides)
 
         wd_codes = keep.tile([P, PACK, P], U32, name="wd_codes", align_bytes=64)
         wd_scales = keep.tile([P, PACK, P], U8, name="wd_scales", align_bytes=64)
@@ -118,10 +122,11 @@ def tile_list_msg_silu_noneP_kernel(
 
         def hidden(c, tag):
             act = keep.tile([P, PACK, EDGES], F32, name="act")
-            for pair in (0, 1):
-                bank = psum.tile([P, 2, EDGES], F32, name="a_bank%d" % pair)
-                for u in (0, 1):
-                    t = 2 * pair + u
+            share = 1 if c == 0 else 2
+            for low in range(0, PACK, share):
+                bank = psum.tile([P, share, EDGES], F32, name="a_bank%d" % (low // share % 2))
+                for u in range(share):
+                    t = low + u
                     for side in (0, 1):
                         nc.tensor.matmul_mx(
                             out=bank[:, u, :],
@@ -132,7 +137,7 @@ def tile_list_msg_silu_noneP_kernel(
                             start=(side == 0),
                             stop=(side == 1),
                         )
-                nc.scalar.activation(act[:, 2 * pair : 2 * pair + 2, :], bank[:], SILU)
+                nc.scalar.activation(act[:, low : low + share, :], bank[:], SILU)
             h_rows = keep.tile([P, PACK, EDGES], BF16, name="h_rows%d" % c, tag="after_h_rows%d" % c, align_bytes=64)
             for t in range(PACK):
                 nc.scalar.activation(h_rows[:, t, :], act[:, t, :], COPY, scale=sm_cols[t])
@@ -173,33 +178,33 @@ def tile_list_msg_silu_noneP_kernel(
                     MULT,
                 )
 
-        gather_scales(0, 1, "after_first_sums")
-        gather_scales(1, 1, "scales_second")
-        gather_words(0, 1, "words_first")
+        gather_scales(0, 2, "scales_first")
         nc.vector.tensor_copy(
             out=w_codes[:].rearrange("p w t (b c) -> p w t b c", c=RUN),
             in_=w_raw[:].rearrange("p w (b t c) -> p w t b c", t=PACK, c=RUN),
         )
-        wd_raw = keep.tile([P, PACK, N], F32, name="wd_raw", tag="after_words")
-        for t in range(PACK):
-            nc.sync.dma_start(out=wd_raw[:, t, :], in_=wd.rearrange("(b t c) n -> t b c n", t=PACK, c=RUN)[t])
+        gather_words(0, 1, "words_first")
         nc.vector.tensor_copy(
             out=w_scales[:].rearrange("p t m -> p (t m)").bitcast(I32).rearrange("p (t b c) -> p t b c", t=PACK, c=RUN // 4),
             in_=w_plane[:].bitcast(I32).rearrange("p (b t c) -> p t b c", t=PACK, c=RUN // 4),
         )
-        gather_words(1, 2, "after_weights")
-        hidden(0, "after_first_h")
-        gather_scales(2, 1, "after_first_sums")
+        gather_words(1, 3, "after_weights")
+        gather_scales(2, 1, "words_first", (0,))
         prepare_wd()
-        wgo_sb = keep.tile([P, J], F32, name="wgo_sb", tag="words_first", align_bytes=64)
-        nc.sync.dma_start(out=wgo_sb[:], in_=wgo)
-        gather_words(3, 1, "after_first_h")
-        gather_scales(3, 1, "after_h_rows0")
-        messages((0, 1), 0, EDGES, "y_pair", "y_pair0")
+        hidden(0, "after_first_h")
+        late = keep.tile([P, 3, EDGES], U8, name="late_scales", tag="after_first_h", align_bytes=64)
+        for u, (c, side) in enumerate(((2, 1), (3, 0), (3, 1))):
+            nc.vector.tensor_copy(
+                late[:, u, :], tab_plane[:].indirect(lists[side][:, c * LIST_COLS : (c + 1) * LIST_COLS])
+            )
+            picked_scales[c, side] = late[:, u, :]
+        messages((0,), 0, EDGES, "y_first", "y0_0")
+        messages((1,), 0, EDGES, "y_one", "y1_0")
         for c in range(1, CHUNKS):
             hidden(c, "h_grouped%d" % c)
             messages((2,), (c - 1) * EDGES, EDGES, "y_one", "after_h_rows%d" % c)
-            messages((0, 1), c * EDGES, EDGES, "y_pair", "y_pair%d" % c)
+            messages((0,), c * EDGES, EDGES, "y_first", "y0_%d" % c)
+            messages((1,), c * EDGES, EDGES, "y_one", "y1_%d" % c)
         messages((2,), (CHUNKS - 1) * EDGES, EDGES, "y_one", "y_third_last")
         messages((3,), 0, J, "y_one", "y_fourth")
 

@@ -23,11 +23,9 @@ EDGES = 256
 CHUNKS = J // EDGES
 LIST_COLS = EDGES // 16
 GROUP = 512
-CLOSING = (
-    [(128, "rows"), (128, "pairs")]
-    + [(256, "pairs")] * 5
-    + [(128, "pairs"), (256, "pairs on Scalar"), (128, "pairs on Scalar")]
-)
+BLOCK = 128
+LAST = 384
+WIDTHS = [128, 128, 256, 256, 256, 256, 256, 128, 256, 128]
 BANK = 512
 
 
@@ -58,9 +56,9 @@ def tile_list_msg_silu_noneP_kernel(
         dst_list = keep.tile([P, J // 16], U16, name="dst_list")
         nc.sync.dma_start(src_list[:], offs)
         nc.sync.dma_start(dst_list[:], offs2)
-        load_scale_rows(tab_plane, 0, tab_scales, range(4))
         w_raw = keep.tile([P, 2, R], I32, name="w_raw")
         nc.sync.dma_start(out=w_raw[:, 0, :], in_=words_of(ws_words))
+        load_scale_rows(tab_plane, 0, tab_scales, range(4))
         nc.sync.dma_start(out=w_raw[:, 1, :], in_=words_of(wt_words))
         load_scale_rows(w_plane, 0, ws_scales, range(1))
         tab_sb = keep.tile([P, T], I32, name="tab_sb", align_bytes=64)
@@ -205,46 +203,37 @@ def tile_list_msg_silu_noneP_kernel(
             messages((2,), (c - 1) * EDGES, EDGES, "y_one", "after_h_rows%d" % c)
             messages((0,), c * EDGES, EDGES, "y_first", "y0_%d" % c)
             messages((1,), c * EDGES, EDGES, "y_one", "y1_%d" % c)
-        messages((2,), (CHUNKS - 1) * EDGES, EDGES, "y_one", "y_third_last")
-        messages((3,), 0, J, "y_one", "y_fourth")
+        messages((2,), (CHUNKS - 1) * EDGES, EDGES, "a_bank0", "y_third_last")
+        messages((3,), 0, J, "a_bank1", "y_fourth")
 
         out_rows = out_0.rearrange("(p i) t -> i p t", i=PACK)
-        pieces = []
-        start = 0
-        for width, kind in CLOSING:
-            cols = slice(start, start + width)
-            if kind == "rows":
-                staged = keep.tile([P, PACK, width], BF16, name="rows%d" % start)
-                places = [staged[:, i, :] for i in range(PACK)]
-            else:
-                staged = keep.tile([P, 2, width, 2], BF16, name="pairs%d" % start)
-                places = [staged[:, i // 2, :, i % 2] for i in range(PACK)]
-            pieces.append((cols, kind, staged, places))
-            start = cols.stop
+        pairs = keep.tile([P, T * PACK], BF16, name="pairs", align_bytes=64)
+
+        def paired(cols):
+            return pairs[:, cols.start * PACK : cols.stop * PACK]
+
+        def round_into_pairs(i, cols):
+            nc.scalar.copy(
+                out=paired(cols).rearrange("p (b u c v) -> p b u c v", u=2, c=BLOCK, v=2)[:, :, i // 2, :, i % 2],
+                in_=pages[i][:, cols].rearrange("p (b c) -> p b c", c=BLOCK),
+            )
+
         for i in range(PACK):
             nc.sync.dma_start(out=out_rows[i], in_=pages[i][:])
             if i < PACK - 1:
-                for cols, kind, staged, places in pieces:
-                    nc.scalar.copy(out=places[i], in_=pages[i][:, cols])
+                round_into_pairs(i, slice(0, T))
         out_scales = keep.tile([P, GROUP], U8, name="out_scales", align_bytes=64)
         out_words = out_1[0].rearrange("p c i -> p (c i)").bitcast(I32)
         out_codes = [keep.tile([P, GROUP], I32, name="out_codes%d" % g, align_bytes=64) for g in range(T // GROUP)]
 
-        def interleave(cols, kind, staged, places):
+        def interleave(cols):
             grouped = keep.tile([P, cols.stop - cols.start, PACK], BF16, name="grouped%d" % cols.start, align_bytes=64)
-            if kind == "rows":
-                nc.vector.tensor_copy(out=places[PACK - 1], in_=pages[PACK - 1][:, cols])
-                nc.vector.tensor_copy(
-                    out=grouped[:].rearrange("p (e f) t -> p e t f", f=4),
-                    in_=staged[:].rearrange("p t (e f) -> p e t f", f=4),
-                )
-            else:
-                nc.scalar.copy(out=places[PACK - 1], in_=pages[PACK - 1][:, cols])
-                move, word = (nc.vector.tensor_copy, I32) if kind == "pairs" else (nc.scalar.copy, U32)
-                move(
-                    out=grouped[:].rearrange("p c t -> p (c t)").bitcast(word).rearrange("p (c u) -> p c u", u=2),
-                    in_=staged[:].rearrange("p u c v -> p (u c v)").bitcast(word).rearrange("p (u c) -> p c u", u=2),
-                )
+            round_into_pairs(PACK - 1, cols)
+            move, word = (nc.vector.tensor_copy, I32) if cols.start < T - LAST else (nc.scalar.copy, U32)
+            move(
+                out=grouped[:].rearrange("p c t -> p (c t)").bitcast(word).rearrange("p (b c u) -> p b c u", c=BLOCK, u=2),
+                in_=paired(cols).bitcast(word).rearrange("p (b u c) -> p b c u", c=BLOCK, u=2),
+            )
             return grouped
 
         def quantise(cols, grouped):
@@ -260,12 +249,14 @@ def tile_list_msg_silu_noneP_kernel(
             elif inside.stop == GROUP:
                 nc.sync.dma_start(out=out_words[:, g * GROUP : (g + 1) * GROUP], in_=out_codes[g][:])
 
-        ready = interleave(*pieces[0])
-        for k, piece in enumerate(pieces):
+        edges = [sum(WIDTHS[:k]) for k in range(len(WIDTHS) + 1)]
+        pieces = [slice(low, high) for low, high in zip(edges, edges[1:])]
+        ready = interleave(pieces[0])
+        for k, cols in enumerate(pieces):
             done = ready
             if k + 1 < len(pieces):
-                ready = interleave(*pieces[k + 1])
-            quantise(piece[0], done)
+                ready = interleave(pieces[k + 1])
+            quantise(cols, done)
         for quad in range(4):
             (nc.scalar if quad % 2 else nc.sync).dma_start(
                 out=out_2[0, 4 * quad : 4 * quad + 4, :].bitcast(I32).rearrange("r (g c) -> g r c", g=4),

@@ -77,9 +77,10 @@ def tile_list_msg_silu_noneP_kernel(
         nc.sync.dma_start(out=wgo_sb[:], in_=wgo)
 
         pages = {}
-        for i in range(PACK):
+        for i in range(PACK - 1):
             pages[i] = keep.tile([P, T], F32, name="page%d" % i)
             nc.vector.memset(pages[i][:].bitcast(I32), 0)
+        pages[PACK - 1] = pages[0]
 
         w_codes = keep.tile([P, 2, PACK, P], I32, name="w_codes", align_bytes=64)
         w_scales = keep.tile([P, PACK, P], U8, name="w_scales", align_bytes=64)
@@ -151,7 +152,7 @@ def tile_list_msg_silu_noneP_kernel(
                 in_=h_grouped[:].rearrange("p e t -> p (e t)"),
             )
 
-        def messages(planes, first, count, bank_name, tag):
+        def messages(planes, first, count, bank_name, tag, between=None):
             y_sb = keep.tile([P, len(planes), count], F32, name="y%d_%d" % (planes[0], first), tag=tag, align_bytes=64)
             width = min(count, BANK // len(planes))
             for start in range(0, count, width):
@@ -168,6 +169,8 @@ def tile_list_msg_silu_noneP_kernel(
                         stop=True,
                     )
                 nc.scalar.copy(out=y_sb[:, :, start : start + width], in_=bank[:])
+            if between is not None:
+                between()
             for u, i in enumerate(planes):
                 nc.vector.tensor_tensor(
                     pages[i][:].indirect(dst_list[:, first // 16 : (first + count) // 16]),
@@ -204,7 +207,6 @@ def tile_list_msg_silu_noneP_kernel(
             messages((0,), c * EDGES, EDGES, "y_first", "y0_%d" % c)
             messages((1,), c * EDGES, EDGES, "y_one", "y1_%d" % c)
         messages((2,), (CHUNKS - 1) * EDGES, EDGES, "a_bank0", "y_third_last")
-        messages((3,), 0, J, "a_bank1", "y_fourth")
 
         out_rows = out_0.rearrange("(p i) t -> i p t", i=PACK)
         pairs = keep.tile([P, T * PACK], BF16, name="pairs", align_bytes=64)
@@ -218,10 +220,13 @@ def tile_list_msg_silu_noneP_kernel(
                 in_=pages[i][:, cols].rearrange("p (b c) -> p b c", c=BLOCK),
             )
 
-        for i in range(PACK):
-            nc.sync.dma_start(out=out_rows[i], in_=pages[i][:])
-            if i < PACK - 1:
+        def hand_out_first_pages():
+            for i in range(PACK - 1):
+                nc.sync.dma_start(out=out_rows[i], in_=pages[i][:])
                 round_into_pairs(i, slice(0, T))
+
+        messages((3,), 0, J, "a_bank1", "y_fourth", hand_out_first_pages)
+        nc.sync.dma_start(out=out_rows[PACK - 1], in_=pages[PACK - 1][:])
         out_scales = keep.tile([P, GROUP], U8, name="out_scales", align_bytes=64)
         out_words = out_1[0].rearrange("p c i -> p (c i)").bitcast(I32)
         out_codes = [keep.tile([P, GROUP], I32, name="out_codes%d" % g, align_bytes=64) for g in range(T // GROUP)]

@@ -19,14 +19,15 @@ MULT = mybir.AluOpType.mult
 P = 128
 PACK = 4
 RUN = 8
+QUADS = 4
+BANK = 512
 EDGES = 256
-CHUNKS = J // EDGES
-LIST_COLS = EDGES // 16
+PER_COLUMN = 16
+SOURCE, TARGET = 0, 1
 GROUP = 512
 BLOCK = 128
-LAST = 384
 WIDTHS = [128, 128, 256, 256, 256, 256, 256, 128, 256, 128]
-BANK = 512
+SCALAR_COLUMNS = 384
 
 
 def tile_list_msg_silu_noneP_kernel(
@@ -37,176 +38,177 @@ def tile_list_msg_silu_noneP_kernel(
         keep = ctx.enter_context(tc.tile_pool(name="keep", bufs=1))
         psum = ctx.enter_context(tc.psum_pool(name="psum", bufs=2))
 
-        def load_scale_rows(plane, first, rows, quads):
+        def load_scale_rows(plane, shift, rows, quads):
             for quad in quads:
                 nc.sync.dma_start(
-                    out=plane[32 * quad + first : 32 * quad + first + 4, :].bitcast(I32),
+                    out=plane[32 * quad + shift : 32 * quad + shift + 4, :].bitcast(I32),
                     in_=rows[0, 4 * quad : 4 * quad + 4, :].bitcast(I32),
                 )
 
         def words_of(packed):
             return packed[0].rearrange("p c i -> p (c i)").bitcast(I32)
 
+        def edges_of(chunk, count=1):
+            return slice(chunk * EDGES, (chunk + count) * EDGES)
+
+        def entries(end, edges):
+            return lists[end][:, edges.start // PER_COLUMN : edges.stop // PER_COLUMN]
+
         tab_plane = keep.tile([P, T], U8, name="tab_plane", align_bytes=64)
-        w_plane = keep.tile([P, R], U8, name="w_plane", tag="after_weights", align_bytes=64)
+        w_plane = keep.tile([P, R], U8, name="w_plane", tag="behind_w_scales", align_bytes=64)
         nc.vector.memset(tab_plane[:].bitcast(I32), 0)
         nc.vector.memset(w_plane[:].bitcast(I32), 0)
 
-        src_list = keep.tile([P, J // 16], U16, name="src_list")
-        dst_list = keep.tile([P, J // 16], U16, name="dst_list")
-        nc.sync.dma_start(src_list[:], offs)
-        nc.sync.dma_start(dst_list[:], offs2)
+        lists = [keep.tile([P, J // PER_COLUMN], U16, name="list%d" % end) for end in (SOURCE, TARGET)]
+        nc.sync.dma_start(lists[SOURCE][:], offs)
+        nc.sync.dma_start(lists[TARGET][:], offs2)
         w_raw = keep.tile([P, 2, R], I32, name="w_raw")
-        nc.sync.dma_start(out=w_raw[:, 0, :], in_=words_of(ws_words))
-        load_scale_rows(tab_plane, 0, tab_scales, range(4))
-        nc.sync.dma_start(out=w_raw[:, 1, :], in_=words_of(wt_words))
-        load_scale_rows(w_plane, 0, ws_scales, range(1))
+        nc.sync.dma_start(out=w_raw[:, SOURCE, :], in_=words_of(ws_words))
+        load_scale_rows(tab_plane, 0, tab_scales, range(QUADS))
+        nc.sync.dma_start(out=w_raw[:, TARGET, :], in_=words_of(wt_words))
+        load_scale_rows(w_plane, 4 * SOURCE, ws_scales, range(1))
         tab_sb = keep.tile([P, T], I32, name="tab_sb", align_bytes=64)
         nc.sync.dma_start(out=tab_sb[:], in_=words_of(tab_words))
-        load_scale_rows(w_plane, 0, ws_scales, range(1, 4))
-        load_scale_rows(w_plane, 4, wt_scales, range(4))
-        sm_sb = keep.tile([P, PACK, RUN], F32, name="sm_sb")
-        sm_cols = [sm_sb[:, t, 0:1] for t in range(PACK)]
+        load_scale_rows(w_plane, 4 * SOURCE, ws_scales, range(1, QUADS))
+        load_scale_rows(w_plane, 4 * TARGET, wt_scales, range(QUADS))
+        sm_sb = keep.tile([P, PACK, 8], F32, name="sm_sb")
         with nc.allow_non_contiguous_dma(reason="one factor for each partition"):
             for t in range(PACK):
-                nc.sync.dma_start(out=sm_cols[t], in_=sm.rearrange("(b t c o) -> t b c o", t=PACK, c=RUN, o=1)[t])
+                nc.sync.dma_start(
+                    out=sm_sb[:, t, 0:1], in_=sm.rearrange("(b t c o) -> t b c o", t=PACK, c=RUN, o=1)[t]
+                )
         wd_raw = keep.tile([P, PACK, N], F32, name="wd_raw")
         for t in range(PACK):
             nc.sync.dma_start(out=wd_raw[:, t, :], in_=wd.rearrange("(b t c) n -> t b c n", t=PACK, c=RUN)[t])
         wgo_sb = keep.tile([P, J], F32, name="wgo_sb", align_bytes=64)
         nc.sync.dma_start(out=wgo_sb[:], in_=wgo)
 
-        pages = {}
-        for i in range(PACK - 1):
-            pages[i] = keep.tile([P, T], F32, name="page%d" % i)
-            nc.vector.memset(pages[i][:].bitcast(I32), 0)
-        pages[PACK - 1] = pages[0]
+        pages = [keep.tile([P, T], F32, name="page%d" % i) for i in range(PACK - 1)]
+        for page in pages:
+            nc.vector.memset(page[:].bitcast(I32), 0)
+        pages.append(pages[0])
+
+        picked_words, picked_scales = {}, {}
+
+        def gather(window, dtype, picked, looks, count, tag):
+            got = keep.tile([P, len(looks), count * EDGES], dtype, name="picked_" + tag, tag=tag, align_bytes=64)
+            for u, (chunk, end) in enumerate(looks):
+                nc.vector.tensor_copy(got[:, u, :], window.indirect(entries(end, edges_of(chunk, count))))
+                for c in range(count):
+                    picked[chunk + c, end] = got[:, u, edges_of(c)]
+
+        def gather_words(looks, count, tag):
+            gather(tab_sb[:].bitcast(U32), U32, picked_words, looks, count, tag)
+
+        def gather_scales(looks, count, tag):
+            gather(tab_plane[:], U8, picked_scales, looks, count, tag)
 
         w_codes = keep.tile([P, 2, PACK, P], I32, name="w_codes", align_bytes=64)
         w_scales = keep.tile([P, PACK, P], U8, name="w_scales", align_bytes=64)
-        lists = (src_list, dst_list)
-        picked_words, picked_scales = {}, {}
-
-        def gather(window, dtype, picked, first, count, tag, sides):
-            got = keep.tile([P, len(sides), count * EDGES], dtype, name="%s_%d" % (tag, first), tag=tag, align_bytes=64)
-            for u, side in enumerate(sides):
-                nc.vector.tensor_copy(
-                    got[:, u, :], window.indirect(lists[side][:, first * LIST_COLS : (first + count) * LIST_COLS])
-                )
-                for c in range(count):
-                    picked[first + c, side] = got[:, u, c * EDGES : (c + 1) * EDGES]
-
-        def gather_words(first, count, tag, sides=(0, 1)):
-            gather(tab_sb[:].bitcast(U32), U32, picked_words, first, count, tag, sides)
-
-        def gather_scales(first, count, tag, sides=(0, 1)):
-            gather(tab_plane[:], U8, picked_scales, first, count, tag, sides)
-
         wd_codes = keep.tile([P, PACK, P], U32, name="wd_codes", align_bytes=64)
         wd_scales = keep.tile([P, PACK, P], U8, name="wd_scales", align_bytes=64)
-
-        def prepare_wd():
-            grouped = keep.tile([P, PACK, P, PACK], BF16, name="wd_grouped", align_bytes=64)
-            nc.vector.tensor_copy(
-                out=grouped[:].rearrange("p i m j -> p m j i"), in_=wd_raw[:].rearrange("p j (m i) -> p m j i", i=PACK)
-            )
-            nc.vector.quantize_mx(
-                out=wd_codes[:].rearrange("p i m -> p (i m)").bitcast(FP8X4),
-                scales=wd_scales[:].rearrange("p i m -> p (i m)"),
-                in_=grouped[:].rearrange("p i m j -> p (i m j)"),
-            )
-
         h_codes = keep.tile([P, J], U32, name="h_codes", align_bytes=64)
         h_scales = keep.tile([P, J], U8, name="h_scales", align_bytes=64)
 
-        def hidden(c, tag):
-            act = keep.tile([P, PACK, EDGES], F32, name="act")
-            share = 1 if c == 0 else 2
+        def activate(chunk):
+            act = keep.tile([P, PACK, EDGES], F32, name="act", tag="behind_act", align_bytes=64)
+            share = 1 if chunk == 0 else BANK // EDGES
             for low in range(0, PACK, share):
                 bank = psum.tile([P, share, EDGES], F32, name="a_bank%d" % (low // share % 2))
                 for u in range(share):
-                    t = low + u
-                    for side in (0, 1):
+                    for end in (SOURCE, TARGET):
                         nc.tensor.matmul_mx(
                             out=bank[:, u, :],
-                            lhsT=w_codes[:, side, t, :].bitcast(FP8X4),
-                            lhsT_scale=w_scales[4 * side :, t, :],
-                            rhs=picked_words[c, side].bitcast(FP8X4),
-                            rhs_scale=picked_scales[c, side],
-                            start=(side == 0),
-                            stop=(side == 1),
+                            lhsT=w_codes[:, end, low + u, :].bitcast(FP8X4),
+                            lhsT_scale=w_scales[4 * end :, low + u, :],
+                            rhs=picked_words[chunk, end].bitcast(FP8X4),
+                            rhs_scale=picked_scales[chunk, end],
+                            start=(end == SOURCE),
+                            stop=(end == TARGET),
                         )
                 nc.scalar.activation(act[:, low : low + share, :], bank[:], SILU)
-            h_rows = keep.tile([P, PACK, EDGES], BF16, name="h_rows%d" % c, tag="after_h_rows%d" % c, align_bytes=64)
+            h_rows = keep.tile([P, PACK, EDGES], BF16, name="h_rows", tag="behind_h_rows%d" % chunk, align_bytes=64)
             for t in range(PACK):
-                nc.scalar.activation(h_rows[:, t, :], act[:, t, :], COPY, scale=sm_cols[t])
-            h_grouped = keep.tile([P, EDGES, PACK], BF16, name="h_grouped%d" % c, tag=tag, align_bytes=64)
+                nc.scalar.activation(h_rows[:, t, :], act[:, t, :], COPY, scale=sm_sb[:, t, 0:1])
+            return h_rows
+
+        def quantise_h(chunk, h_rows):
+            grouped = keep.tile([P, EDGES, PACK], BF16, name="h_grouped", tag="behind_h%d" % chunk, align_bytes=64)
             nc.scalar.copy(
-                out=h_grouped[:].rearrange("p (e f) t -> p e t f", f=4),
+                out=grouped[:].rearrange("p (e f) t -> p e t f", f=4),
                 in_=h_rows[:].rearrange("p t (e f) -> p e t f", f=4),
             )
-            cols = slice(c * EDGES, (c + 1) * EDGES)
             nc.vector.quantize_mx(
-                out=h_codes[:, cols].bitcast(FP8X4),
-                scales=h_scales[:, cols],
-                in_=h_grouped[:].rearrange("p e t -> p (e t)"),
+                out=h_codes[:, edges_of(chunk)].bitcast(FP8X4),
+                scales=h_scales[:, edges_of(chunk)],
+                in_=grouped[:].rearrange("p e t -> p (e t)"),
             )
 
-        def messages(planes, first, count, bank_name, tag, between=None):
-            y_sb = keep.tile([P, len(planes), count], F32, name="y%d_%d" % (planes[0], first), tag=tag, align_bytes=64)
-            width = min(count, BANK // len(planes))
-            for start in range(0, count, width):
-                cols = slice(first + start, first + start + width)
-                bank = psum.tile([P, len(planes), width], F32, name=bank_name)
-                for u, i in enumerate(planes):
-                    nc.tensor.matmul_mx(
-                        out=bank[:, u, :],
-                        lhsT=wd_codes[:, i, :].bitcast(FP8X4),
-                        lhsT_scale=wd_scales[:, i, :],
-                        rhs=h_codes[:, cols].bitcast(FP8X4),
-                        rhs_scale=h_scales[:, cols],
-                        start=True,
-                        stop=True,
-                    )
-                nc.scalar.copy(out=y_sb[:, :, start : start + width], in_=bank[:])
-            if between is not None:
-                between()
-            for u, i in enumerate(planes):
-                nc.vector.tensor_tensor(
-                    pages[i][:].indirect(dst_list[:, first // 16 : (first + count) // 16]),
-                    y_sb[:, u, :],
-                    wgo_sb[:, first : first + count],
-                    MULT,
+        def messages(i, edges, bank_name, tag=None):
+            name = "y%d_%d" % (i, edges.start)
+            y = keep.tile([P, edges.stop - edges.start], F32, name=name, tag=tag or name, align_bytes=64)
+            width = min(edges.stop - edges.start, BANK)
+            for start in range(edges.start, edges.stop, width):
+                bank = psum.tile([P, width], F32, name=bank_name)
+                nc.tensor.matmul_mx(
+                    out=bank[:],
+                    lhsT=wd_codes[:, i, :].bitcast(FP8X4),
+                    lhsT_scale=wd_scales[:, i, :],
+                    rhs=h_codes[:, start : start + width].bitcast(FP8X4),
+                    rhs_scale=h_scales[:, start : start + width],
+                    start=True,
+                    stop=True,
                 )
+                nc.scalar.copy(out=y[:, start - edges.start : start - edges.start + width], in_=bank[:])
+            return y
 
-        gather_scales(0, 2, "scales_first")
+        def scatter(i, edges, y):
+            nc.vector.tensor_tensor(pages[i][:].indirect(entries(TARGET, edges)), y[:], wgo_sb[:, edges], MULT)
+
+        def send(i, edges, bank_name, tag=None):
+            scatter(i, edges, messages(i, edges, bank_name, tag))
+
+        gather_scales([(0, SOURCE), (0, TARGET)], 2, "first_scales")
         nc.vector.tensor_copy(
             out=w_codes[:].rearrange("p w t (b c) -> p w t b c", c=RUN),
             in_=w_raw[:].rearrange("p w (b t c) -> p w t b c", t=PACK, c=RUN),
         )
-        gather_words(0, 1, "words_first")
+        gather_words([(0, SOURCE), (0, TARGET)], 1, "behind_first_sums")
         nc.vector.tensor_copy(
             out=w_scales[:].rearrange("p t m -> p (t m)").bitcast(I32).rearrange("p (t b c) -> p t b c", t=PACK, c=RUN // 4),
             in_=w_plane[:].bitcast(I32).rearrange("p (b t c) -> p t b c", t=PACK, c=RUN // 4),
         )
-        gather_words(1, 3, "after_weights")
-        gather_scales(2, 1, "words_first", (0,))
-        prepare_wd()
-        hidden(0, "after_first_h")
-        late = keep.tile([P, 3, EDGES], U8, name="late_scales", tag="after_first_h", align_bytes=64)
-        for u, (c, side) in enumerate(((2, 1), (3, 0), (3, 1))):
-            nc.vector.tensor_copy(
-                late[:, u, :], tab_plane[:].indirect(lists[side][:, c * LIST_COLS : (c + 1) * LIST_COLS])
-            )
-            picked_scales[c, side] = late[:, u, :]
-        messages((0,), 0, EDGES, "y_first", "y0_0")
-        messages((1,), 0, EDGES, "y_one", "y1_0")
-        for c in range(1, CHUNKS):
-            hidden(c, "h_grouped%d" % c)
-            messages((2,), (c - 1) * EDGES, EDGES, "y_one", "after_h_rows%d" % c)
-            messages((0,), c * EDGES, EDGES, "y_first", "y0_%d" % c)
-            messages((1,), c * EDGES, EDGES, "y_one", "y1_%d" % c)
-        messages((2,), (CHUNKS - 1) * EDGES, EDGES, "a_bank0", "y_third_last")
+
+        gather_words([(1, SOURCE), (1, TARGET)], 3, "behind_w_scales")
+        gather_scales([(2, SOURCE)], 1, "behind_first_sums")
+        wd_grouped = keep.tile([P, PACK, P, PACK], BF16, name="wd_grouped", align_bytes=64)
+        nc.vector.tensor_copy(
+            out=wd_grouped[:].rearrange("p i m t -> p m t i"), in_=wd_raw[:].rearrange("p t (m i) -> p m t i", i=PACK)
+        )
+        nc.vector.quantize_mx(
+            out=wd_codes[:].rearrange("p i m -> p (i m)").bitcast(FP8X4),
+            scales=wd_scales[:].rearrange("p i m -> p (i m)"),
+            in_=wd_grouped[:].rearrange("p i m t -> p (i m t)"),
+        )
+
+        quantise_h(0, activate(0))
+        gather_scales([(2, TARGET), (3, SOURCE), (3, TARGET)], 1, "behind_h0")
+        send(0, edges_of(0), "y_first")
+        send(1, edges_of(0), "y_other")
+        quantise_h(1, activate(1))
+        send(2, edges_of(0), "y_other", "behind_h_rows1")
+        send(0, edges_of(1), "y_first")
+        send(1, edges_of(1), "y_other")
+        quantise_h(2, activate(2))
+        send(2, edges_of(1), "y_other", "behind_h_rows2")
+        last_rows = activate(3)
+        send(0, edges_of(2), "y_first", "behind_act")
+        quantise_h(3, last_rows)
+        send(1, edges_of(2), "y_other", "behind_h_rows3")
+        send(0, edges_of(3), "y_first")
+        send(1, edges_of(3), "y_other")
+        send(2, edges_of(2, 2), "a_bank0")
+        last_messages = messages(3, slice(0, J), "a_bank1")
 
         out_rows = out_0.rearrange("(p i) t -> i p t", i=PACK)
         pairs = keep.tile([P, T * PACK], BF16, name="pairs", align_bytes=64)
@@ -220,50 +222,46 @@ def tile_list_msg_silu_noneP_kernel(
                 in_=pages[i][:, cols].rearrange("p (b c) -> p b c", c=BLOCK),
             )
 
-        def hand_out_first_pages():
-            for i in range(PACK - 1):
-                nc.sync.dma_start(out=out_rows[i], in_=pages[i][:])
-                round_into_pairs(i, slice(0, T))
-
-        messages((3,), 0, J, "a_bank1", "y_fourth", hand_out_first_pages)
+        for i in range(PACK - 1):
+            nc.sync.dma_start(out=out_rows[i], in_=pages[i][:])
+            round_into_pairs(i, slice(0, T))
+        scatter(PACK - 1, slice(0, J), last_messages)
         nc.sync.dma_start(out=out_rows[PACK - 1], in_=pages[PACK - 1][:])
-        out_scales = keep.tile([P, GROUP], U8, name="out_scales", align_bytes=64)
-        out_words = out_1[0].rearrange("p c i -> p (c i)").bitcast(I32)
+
+        out_plane = keep.tile([P, GROUP], U8, name="out_plane", align_bytes=64)
         out_codes = [keep.tile([P, GROUP], I32, name="out_codes%d" % g, align_bytes=64) for g in range(T // GROUP)]
+        out_words = words_of(out_1)
 
         def interleave(cols):
-            grouped = keep.tile([P, cols.stop - cols.start, PACK], BF16, name="grouped%d" % cols.start, align_bytes=64)
+            grouped = keep.tile([P, (cols.stop - cols.start) * PACK], BF16, name="grouped%d" % cols.start, align_bytes=64)
             round_into_pairs(PACK - 1, cols)
-            move, word = (nc.vector.tensor_copy, I32) if cols.start < T - LAST else (nc.scalar.copy, U32)
+            move, word = (nc.vector.tensor_copy, I32) if cols.start < T - SCALAR_COLUMNS else (nc.scalar.copy, U32)
             move(
-                out=grouped[:].rearrange("p c t -> p (c t)").bitcast(word).rearrange("p (b c u) -> p b c u", c=BLOCK, u=2),
+                out=grouped[:].bitcast(word).rearrange("p (b c u) -> p b c u", c=BLOCK, u=2),
                 in_=paired(cols).bitcast(word).rearrange("p (b u c) -> p b c u", c=BLOCK, u=2),
             )
             return grouped
 
-        def quantise(cols, grouped):
+        def quantise_out(cols, grouped):
             g = cols.start // GROUP
             inside = slice(cols.start - g * GROUP, cols.stop - g * GROUP)
             nc.vector.quantize_mx(
-                out=out_codes[g][:, inside].bitcast(FP8X4),
-                scales=out_scales[4 * g :, inside],
-                in_=grouped[:].rearrange("p c t -> p (c t)"),
+                out=out_codes[g][:, inside].bitcast(FP8X4), scales=out_plane[4 * g :, inside], in_=grouped[:]
             )
             if g == T // GROUP - 1:
                 nc.sync.dma_start(out=out_words[:, cols], in_=out_codes[g][:, inside])
             elif inside.stop == GROUP:
                 nc.sync.dma_start(out=out_words[:, g * GROUP : (g + 1) * GROUP], in_=out_codes[g][:])
 
-        edges = [sum(WIDTHS[:k]) for k in range(len(WIDTHS) + 1)]
-        pieces = [slice(low, high) for low, high in zip(edges, edges[1:])]
-        ready = interleave(pieces[0])
+        pieces = [slice(sum(WIDTHS[:k]), sum(WIDTHS[: k + 1])) for k in range(len(WIDTHS))]
+        ahead = interleave(pieces[0])
         for k, cols in enumerate(pieces):
-            done = ready
+            current = ahead
             if k + 1 < len(pieces):
-                ready = interleave(pieces[k + 1])
-            quantise(cols, done)
-        for quad in range(4):
+                ahead = interleave(pieces[k + 1])
+            quantise_out(cols, current)
+        for quad in range(QUADS):
             (nc.scalar if quad % 2 else nc.sync).dma_start(
-                out=out_2[0, 4 * quad : 4 * quad + 4, :].bitcast(I32).rearrange("r (g c) -> g r c", g=4),
-                in_=out_scales[32 * quad : 32 * quad + 16, :].bitcast(I32),
+                out=out_2[0, 4 * quad : 4 * quad + 4, :].bitcast(I32).rearrange("s (g c) -> g s c", g=T // GROUP),
+                in_=out_plane[32 * quad : 32 * quad + 16, :].bitcast(I32),
             )

@@ -65,10 +65,10 @@ def tile_list_msg_silu_noneP_kernel(
         w_raw = keep.tile([P, 2, R], I32, name="w_raw")
         nc.sync.dma_start(out=w_raw[:, SOURCE, :], in_=words_of(ws_words))
         load_scale_rows(tab_plane, 0, tab_scales, range(QUADS))
-        nc.sync.dma_start(out=w_raw[:, TARGET, :], in_=words_of(wt_words))
-        load_scale_rows(w_plane, 4 * SOURCE, ws_scales, range(1))
         tab_sb = keep.tile([P, T], I32, name="tab_sb", align_bytes=64)
         nc.sync.dma_start(out=tab_sb[:], in_=words_of(tab_words))
+        load_scale_rows(w_plane, 4 * SOURCE, ws_scales, range(1))
+        nc.sync.dma_start(out=w_raw[:, TARGET, :], in_=words_of(wt_words))
         load_scale_rows(w_plane, 4 * SOURCE, ws_scales, range(1, QUADS))
         load_scale_rows(w_plane, 4 * TARGET, wt_scales, range(QUADS))
         sm_sb = keep.tile([P, PACK, 8], F32, name="sm_sb")
@@ -133,7 +133,7 @@ def tile_list_msg_silu_noneP_kernel(
             return h_rows
 
         def quantise_h(chunk, h_rows):
-            grouped = keep.tile([P, EDGES, PACK], BF16, name="h_grouped", tag="behind_h%d" % chunk, align_bytes=64)
+            grouped = keep.tile([P, EDGES, PACK], BF16, name="h_grouped%d" % chunk, align_bytes=64)
             nc.scalar.copy(
                 out=grouped[:].rearrange("p (e f) t -> p e t f", f=4),
                 in_=h_rows[:].rearrange("p t (e f) -> p e t f", f=4),
@@ -168,12 +168,16 @@ def tile_list_msg_silu_noneP_kernel(
         def send(i, edges, bank_name, tag=None):
             scatter(i, edges, messages(i, edges, bank_name, tag))
 
+        def deal_words(end):
+            nc.vector.tensor_copy(
+                out=w_codes[:, end].rearrange("p t (b c) -> p t b c", c=RUN),
+                in_=w_raw[:, end, :].rearrange("p (b t c) -> p t b c", t=PACK, c=RUN),
+            )
+
+        deal_words(SOURCE)
         gather_scales([(0, SOURCE), (0, TARGET)], 2, "first_scales")
-        nc.vector.tensor_copy(
-            out=w_codes[:].rearrange("p w t (b c) -> p w t b c", c=RUN),
-            in_=w_raw[:].rearrange("p w (b t c) -> p w t b c", t=PACK, c=RUN),
-        )
         gather_words([(0, SOURCE), (0, TARGET)], 1, "behind_first_sums")
+        deal_words(TARGET)
         nc.vector.tensor_copy(
             out=w_scales[:].rearrange("p t m -> p (t m)").bitcast(I32).rearrange("p (t b c) -> p t b c", t=PACK, c=RUN // 4),
             in_=w_plane[:].bitcast(I32).rearrange("p (b t c) -> p t b c", t=PACK, c=RUN // 4),
@@ -192,7 +196,7 @@ def tile_list_msg_silu_noneP_kernel(
         )
 
         quantise_h(0, activate(0))
-        gather_scales([(2, TARGET), (3, SOURCE), (3, TARGET)], 1, "behind_h0")
+        gather_scales([(2, TARGET), (3, SOURCE), (3, TARGET)], 1, "behind_h_rows0")
         send(0, edges_of(0), "y_first")
         send(1, edges_of(0), "y_other")
         quantise_h(1, activate(1))

@@ -62,13 +62,13 @@ def tile_list_msg_silu_noneP_kernel(
         lists = [keep.tile([P, J // PER_COLUMN], U16, name="list%d" % end) for end in (SOURCE, TARGET)]
         nc.sync.dma_start(lists[SOURCE][:], offs)
         nc.sync.dma_start(lists[TARGET][:], offs2)
-        w_raw = keep.tile([P, 2, R], I32, name="w_raw")
-        nc.sync.dma_start(out=w_raw[:, SOURCE, :], in_=words_of(ws_words))
+        w_raw = [keep.tile([P, R], I32, name="ws_raw", tag="behind_ws"), keep.tile([P, R], I32, name="wt_raw")]
+        nc.sync.dma_start(out=w_raw[SOURCE][:], in_=words_of(ws_words))
         load_scale_rows(tab_plane, 0, tab_scales, range(QUADS))
         tab_sb = keep.tile([P, T], I32, name="tab_sb", align_bytes=64)
         nc.sync.dma_start(out=tab_sb[:], in_=words_of(tab_words))
         load_scale_rows(w_plane, 4 * SOURCE, ws_scales, range(1))
-        nc.sync.dma_start(out=w_raw[:, TARGET, :], in_=words_of(wt_words))
+        nc.sync.dma_start(out=w_raw[TARGET][:], in_=words_of(wt_words))
         load_scale_rows(w_plane, 4 * SOURCE, ws_scales, range(1, QUADS))
         load_scale_rows(w_plane, 4 * TARGET, wt_scales, range(QUADS))
         sm_sb = keep.tile([P, PACK, 8], F32, name="sm_sb")
@@ -83,10 +83,9 @@ def tile_list_msg_silu_noneP_kernel(
         wgo_sb = keep.tile([P, J], F32, name="wgo_sb", align_bytes=64)
         nc.sync.dma_start(out=wgo_sb[:], in_=wgo)
 
-        pages = [keep.tile([P, T], F32, name="page%d" % i) for i in range(PACK - 1)]
+        pages = [keep.tile([P, T], F32, name="page%d" % i) for i in range(PACK - 2)]
         for page in pages:
             nc.vector.memset(page[:].bitcast(I32), 0)
-        pages.append(pages[0])
 
         picked_words, picked_scales = {}, {}
 
@@ -171,10 +170,13 @@ def tile_list_msg_silu_noneP_kernel(
         def deal_words(end):
             nc.vector.tensor_copy(
                 out=w_codes[:, end].rearrange("p t (b c) -> p t b c", c=RUN),
-                in_=w_raw[:, end, :].rearrange("p (b t c) -> p t b c", t=PACK, c=RUN),
+                in_=w_raw[end][:].rearrange("p (b t c) -> p t b c", t=PACK, c=RUN),
             )
 
         deal_words(SOURCE)
+        pages.append(keep.tile([P, T], F32, name="page2", tag="behind_ws"))
+        nc.gpsimd.memset(pages[2][:].bitcast(I32), 0)
+        pages.append(pages[0])
         gather_scales([(0, SOURCE), (0, TARGET)], 2, "first_scales")
         gather_words([(0, SOURCE), (0, TARGET)], 1, "behind_first_sums")
         deal_words(TARGET)

@@ -65,11 +65,11 @@ def tile_list_msg_silu_noneP_kernel(
         w_raw = [keep.tile([P, R], I32, name="ws_raw", tag="behind_ws"), keep.tile([P, R], I32, name="wt_raw")]
         nc.sync.dma_start(out=w_raw[SOURCE][:], in_=words_of(ws_words))
         load_scale_rows(tab_plane, 0, tab_scales, range(QUADS))
+        load_scale_rows(w_plane, 4 * SOURCE, ws_scales, range(2))
         tab_sb = keep.tile([P, T], I32, name="tab_sb", align_bytes=64)
         nc.sync.dma_start(out=tab_sb[:], in_=words_of(tab_words))
-        load_scale_rows(w_plane, 4 * SOURCE, ws_scales, range(1))
         nc.sync.dma_start(out=w_raw[TARGET][:], in_=words_of(wt_words))
-        load_scale_rows(w_plane, 4 * SOURCE, ws_scales, range(1, QUADS))
+        load_scale_rows(w_plane, 4 * SOURCE, ws_scales, range(2, QUADS))
         load_scale_rows(w_plane, 4 * TARGET, wt_scales, range(QUADS))
         sm_sb = keep.tile([P, PACK, 8], F32, name="sm_sb")
         with nc.allow_non_contiguous_dma(reason="one factor for each partition"):
@@ -177,7 +177,7 @@ def tile_list_msg_silu_noneP_kernel(
         pages.append(keep.tile([P, T], F32, name="page2", tag="behind_ws"))
         nc.gpsimd.memset(pages[2][:].bitcast(I32), 0)
         pages.append(pages[0])
-        gather_scales([(0, SOURCE), (0, TARGET)], 2, "first_scales")
+        gather_scales([(0, SOURCE), (0, TARGET), (2, SOURCE)], 2, "first_scales")
         gather_words([(0, SOURCE), (0, TARGET)], 1, "behind_first_sums")
         deal_words(TARGET)
         nc.vector.tensor_copy(
@@ -186,7 +186,6 @@ def tile_list_msg_silu_noneP_kernel(
         )
 
         gather_words([(1, SOURCE), (1, TARGET)], 3, "behind_w_scales")
-        gather_scales([(2, SOURCE)], 1, "behind_first_sums")
         wd_grouped = keep.tile([P, PACK, P, PACK], BF16, name="wd_grouped", align_bytes=64)
         nc.vector.tensor_copy(
             out=wd_grouped[:].rearrange("p i m t -> p m t i"), in_=wd_raw[:].rearrange("p t (m i) -> p m t i", i=PACK)
@@ -198,7 +197,7 @@ def tile_list_msg_silu_noneP_kernel(
         )
 
         quantise_h(0, activate(0))
-        gather_scales([(2, TARGET), (3, SOURCE), (3, TARGET)], 1, "behind_h_rows0")
+        gather_scales([(2, TARGET)], 2, "behind_h_rows0")
         send(0, edges_of(0), "y_first")
         send(1, edges_of(0), "y_other")
         quantise_h(1, activate(1))

@@ -54,7 +54,7 @@ def tile_list_msg_silu_noneP_kernel(
         def entries(end, edges):
             return lists[end][:, edges.start // PER_COLUMN : edges.stop // PER_COLUMN]
 
-        tab_plane = keep.tile([P, T], U8, name="tab_plane", align_bytes=64)
+        tab_plane = keep.tile([P, T], U8, name="tab_plane", tag="behind_gathers", align_bytes=64)
         w_plane = keep.tile([P, R], U8, name="w_plane", tag="behind_w_scales", align_bytes=64)
         nc.vector.memset(tab_plane[:].bitcast(I32), 0)
         nc.vector.memset(w_plane[:].bitcast(I32), 0)
@@ -62,7 +62,7 @@ def tile_list_msg_silu_noneP_kernel(
         lists = [keep.tile([P, J // PER_COLUMN], U16, name="list%d" % end) for end in (SOURCE, TARGET)]
         nc.sync.dma_start(lists[SOURCE][:], offs)
         nc.sync.dma_start(lists[TARGET][:], offs2)
-        w_raw = [keep.tile([P, R], I32, name="ws_raw", tag="behind_ws"), keep.tile([P, R], I32, name="wt_raw")]
+        w_raw = [keep.tile([P, R], I32, name="ws_raw"), keep.tile([P, R], I32, name="wt_raw")]
         nc.sync.dma_start(out=w_raw[SOURCE][:], in_=words_of(ws_words))
         load_scale_rows(tab_plane, 0, tab_scales, range(QUADS))
         load_scale_rows(w_plane, 4 * SOURCE, ws_scales, range(2))
@@ -174,9 +174,6 @@ def tile_list_msg_silu_noneP_kernel(
             )
 
         deal_words(SOURCE)
-        pages.append(keep.tile([P, T], F32, name="page2", tag="behind_ws"))
-        nc.gpsimd.memset(pages[2][:].bitcast(I32), 0)
-        pages.append(pages[0])
         gather_scales([(0, SOURCE), (0, TARGET), (2, SOURCE)], 2, "first_scales")
         gather_words([(0, SOURCE), (0, TARGET)], 1, "behind_first_sums")
         deal_words(TARGET)
@@ -198,6 +195,9 @@ def tile_list_msg_silu_noneP_kernel(
 
         quantise_h(0, activate(0))
         gather_scales([(2, TARGET)], 2, "behind_h_rows0")
+        pages.append(keep.tile([P, T], F32, name="page2", tag="behind_gathers", align_bytes=64))
+        nc.gpsimd.memset(pages[2][:].bitcast(I32), 0)
+        pages.append(pages[0])
         send(0, edges_of(0), "y_first")
         send(1, edges_of(0), "y_other")
         quantise_h(1, activate(1))

@@ -26,8 +26,10 @@ PER_COLUMN = 16
 SOURCE, TARGET = 0, 1
 GROUP = 512
 BLOCK = 128
-WIDTHS = [128, 128, 256, 256, 256, 256, 256, 128, 256, 128]
-SCALAR_COLUMNS = 384
+WIDTHS = [128, 128, 256, 256, 256, 256, 256, 256, 128, 128]
+SCALAR_COLUMNS = 512
+VECTOR_COLUMNS = 256
+TURNS = [2, 0, 1, 3]
 
 
 def tile_list_msg_silu_noneP_kernel(
@@ -72,14 +74,19 @@ def tile_list_msg_silu_noneP_kernel(
         load_scale_rows(w_plane, 4 * SOURCE, ws_scales, range(2, QUADS))
         load_scale_rows(w_plane, 4 * TARGET, wt_scales, range(QUADS))
         sm_sb = keep.tile([P, PACK, 8], F32, name="sm_sb")
+        wd_raw = keep.tile([P, PACK, N], F32, name="wd_raw")
+
+        def load_wd(slices):
+            for t in slices:
+                nc.sync.dma_start(out=wd_raw[:, t, :], in_=wd.rearrange("(b t c) n -> t b c n", t=PACK, c=RUN)[t])
+
+        load_wd(range(2))
         with nc.allow_non_contiguous_dma(reason="one factor for each partition"):
             for t in range(PACK):
                 nc.sync.dma_start(
                     out=sm_sb[:, t, 0:1], in_=sm.rearrange("(b t c o) -> t b c o", t=PACK, c=RUN, o=1)[t]
                 )
-        wd_raw = keep.tile([P, PACK, N], F32, name="wd_raw")
-        for t in range(PACK):
-            nc.sync.dma_start(out=wd_raw[:, t, :], in_=wd.rearrange("(b t c) n -> t b c n", t=PACK, c=RUN)[t])
+        load_wd(range(2, PACK))
         wgo_sb = keep.tile([P, J], F32, name="wgo_sb", align_bytes=64)
         nc.sync.dma_start(out=wgo_sb[:], in_=wgo)
 
@@ -109,38 +116,54 @@ def tile_list_msg_silu_noneP_kernel(
         h_codes = keep.tile([P, J], U32, name="h_codes", align_bytes=64)
         h_scales = keep.tile([P, J], U8, name="h_scales", align_bytes=64)
 
+        def sums(chunk, slices, bank_name):
+            bank = psum.tile([P, len(slices), EDGES], F32, name=bank_name)
+            for u, t in enumerate(slices):
+                for end in (SOURCE, TARGET):
+                    nc.tensor.matmul_mx(
+                        out=bank[:, u, :],
+                        lhsT=w_codes[:, end, t, :].bitcast(FP8X4),
+                        lhsT_scale=w_scales[4 * end :, t, :],
+                        rhs=picked_words[chunk, end].bitcast(FP8X4),
+                        rhs_scale=picked_scales[chunk, end],
+                        start=(end == SOURCE),
+                        stop=(end == TARGET),
+                    )
+            return bank
+
+        def activate_first():
+            act = keep.tile([P, PACK, EDGES], F32, name="act", tag="behind_act", align_bytes=64)
+            h_pairs = keep.tile([P, 2, EDGES * 2], BF16, name="h_pairs", tag="behind_h_rows0", align_bytes=64)
+            for t in range(PACK):
+                nc.scalar.activation(act[:, t : t + 1, :], sums(0, [t], "a_bank%d" % (t % 2))[:], SILU)
+                nc.scalar.activation(h_pairs[:, t // 2, t % 2 :: 2], act[:, t, :], COPY, scale=sm_sb[:, t, 0:1])
+            grouped = keep.tile([P, EDGES * PACK], BF16, name="h_grouped0", align_bytes=64)
+            nc.scalar.copy(
+                out=grouped[:].bitcast(U32).rearrange("p (e u) -> p e u", u=2),
+                in_=h_pairs[:].rearrange("p u x -> p (u x)").bitcast(U32).rearrange("p (u e) -> p e u", u=2),
+            )
+            return grouped
+
         def activate(chunk):
             act = keep.tile([P, PACK, EDGES], F32, name="act", tag="behind_act", align_bytes=64)
-            share = 1 if chunk == 0 else BANK // EDGES
-            for low in range(0, PACK, share):
-                bank = psum.tile([P, share, EDGES], F32, name="a_bank%d" % (low // share % 2))
-                for u in range(share):
-                    for end in (SOURCE, TARGET):
-                        nc.tensor.matmul_mx(
-                            out=bank[:, u, :],
-                            lhsT=w_codes[:, end, low + u, :].bitcast(FP8X4),
-                            lhsT_scale=w_scales[4 * end :, low + u, :],
-                            rhs=picked_words[chunk, end].bitcast(FP8X4),
-                            rhs_scale=picked_scales[chunk, end],
-                            start=(end == SOURCE),
-                            stop=(end == TARGET),
-                        )
-                nc.scalar.activation(act[:, low : low + share, :], bank[:], SILU)
+            for low in (0, 2):
+                nc.scalar.activation(act[:, low : low + 2, :], sums(chunk, [low, low + 1], "a_bank%d" % (low // 2))[:], SILU)
             h_rows = keep.tile([P, PACK, EDGES], BF16, name="h_rows", tag="behind_h_rows%d" % chunk, align_bytes=64)
             for t in range(PACK):
                 nc.scalar.activation(h_rows[:, t, :], act[:, t, :], COPY, scale=sm_sb[:, t, 0:1])
             return h_rows
 
-        def quantise_h(chunk, h_rows):
-            grouped = keep.tile([P, EDGES, PACK], BF16, name="h_grouped%d" % chunk, align_bytes=64)
+        def group_rows(chunk, h_rows):
+            grouped = keep.tile([P, EDGES * PACK], BF16, name="h_grouped%d" % chunk, align_bytes=64)
             nc.scalar.copy(
-                out=grouped[:].rearrange("p (e f) t -> p e t f", f=4),
+                out=grouped[:].rearrange("p (e f t) -> p e t f", f=4, t=PACK),
                 in_=h_rows[:].rearrange("p t (e f) -> p e t f", f=4),
             )
+            return grouped
+
+        def quantise_h(chunk, grouped):
             nc.vector.quantize_mx(
-                out=h_codes[:, edges_of(chunk)].bitcast(FP8X4),
-                scales=h_scales[:, edges_of(chunk)],
-                in_=grouped[:].rearrange("p e t -> p (e t)"),
+                out=h_codes[:, edges_of(chunk)].bitcast(FP8X4), scales=h_scales[:, edges_of(chunk)], in_=grouped[:]
             )
 
         def messages(i, edges, bank_name, tag=None):
@@ -151,8 +174,8 @@ def tile_list_msg_silu_noneP_kernel(
                 bank = psum.tile([P, width], F32, name=bank_name)
                 nc.tensor.matmul_mx(
                     out=bank[:],
-                    lhsT=wd_codes[:, i, :].bitcast(FP8X4),
-                    lhsT_scale=wd_scales[:, i, :],
+                    lhsT=wd_codes[:, TURNS[i], :].bitcast(FP8X4),
+                    lhsT_scale=wd_scales[:, TURNS[i], :],
                     rhs=h_codes[:, start : start + width].bitcast(FP8X4),
                     rhs_scale=h_scales[:, start : start + width],
                     start=True,
@@ -174,7 +197,8 @@ def tile_list_msg_silu_noneP_kernel(
             )
 
         deal_words(SOURCE)
-        gather_scales([(0, SOURCE), (0, TARGET), (2, SOURCE)], 2, "first_scales")
+        gather_scales([(0, SOURCE), (0, TARGET)], 2, "first_scales")
+        gather_scales([(2, SOURCE)], 1, "third_source_scales")
         gather_words([(0, SOURCE), (0, TARGET)], 1, "behind_first_sums")
         deal_words(TARGET)
         nc.vector.tensor_copy(
@@ -193,22 +217,22 @@ def tile_list_msg_silu_noneP_kernel(
             in_=wd_grouped[:].rearrange("p i m t -> p (i m t)"),
         )
 
-        quantise_h(0, activate(0))
-        gather_scales([(2, TARGET)], 2, "behind_h_rows0")
+        quantise_h(0, activate_first())
+        gather_scales([(2, TARGET), (3, SOURCE), (3, TARGET)], 1, "behind_h_rows0")
         pages.append(keep.tile([P, T], F32, name="page2", tag="behind_gathers", align_bytes=64))
         nc.gpsimd.memset(pages[2][:].bitcast(I32), 0)
         pages.append(pages[0])
         send(0, edges_of(0), "y_first")
         send(1, edges_of(0), "y_other")
-        quantise_h(1, activate(1))
+        quantise_h(1, group_rows(1, activate(1)))
         send(2, edges_of(0), "y_other", "behind_h_rows1")
         send(0, edges_of(1), "y_first")
         send(1, edges_of(1), "y_other")
-        quantise_h(2, activate(2))
+        quantise_h(2, group_rows(2, activate(2)))
         send(2, edges_of(1), "y_other", "behind_h_rows2")
         last_rows = activate(3)
         send(0, edges_of(2), "y_first", "behind_act")
-        quantise_h(3, last_rows)
+        quantise_h(3, group_rows(3, last_rows))
         send(1, edges_of(2), "y_other", "behind_h_rows3")
         send(0, edges_of(3), "y_first")
         send(1, edges_of(3), "y_other")
@@ -221,14 +245,14 @@ def tile_list_msg_silu_noneP_kernel(
         def paired(cols):
             return pairs[:, cols.start * PACK : cols.stop * PACK]
 
-        def round_into_pairs(i, cols):
-            nc.scalar.copy(
-                out=paired(cols).rearrange("p (b u c v) -> p b u c v", u=2, c=BLOCK, v=2)[:, :, i // 2, :, i % 2],
+        def round_into_pairs(i, cols, copy=nc.scalar.copy):
+            copy(
+                out=paired(cols).rearrange("p (b u c v) -> p b u c v", u=2, c=BLOCK, v=2)[:, :, TURNS[i] // 2, :, TURNS[i] % 2],
                 in_=pages[i][:, cols].rearrange("p (b c) -> p b c", c=BLOCK),
             )
 
         for i in range(PACK - 1):
-            nc.sync.dma_start(out=out_rows[i], in_=pages[i][:])
+            nc.sync.dma_start(out=out_rows[TURNS[i]], in_=pages[i][:])
             round_into_pairs(i, slice(0, T))
         scatter(PACK - 1, slice(0, J), last_messages)
         nc.sync.dma_start(out=out_rows[PACK - 1], in_=pages[PACK - 1][:])
@@ -239,7 +263,8 @@ def tile_list_msg_silu_noneP_kernel(
 
         def interleave(cols):
             grouped = keep.tile([P, (cols.stop - cols.start) * PACK], BF16, name="grouped%d" % cols.start, align_bytes=64)
-            round_into_pairs(PACK - 1, cols)
+            if cols.start >= VECTOR_COLUMNS:
+                round_into_pairs(PACK - 1, cols)
             move, word = (nc.vector.tensor_copy, I32) if cols.start < T - SCALAR_COLUMNS else (nc.scalar.copy, U32)
             move(
                 out=grouped[:].bitcast(word).rearrange("p (b c u) -> p b c u", c=BLOCK, u=2),
@@ -259,6 +284,8 @@ def tile_list_msg_silu_noneP_kernel(
                 nc.sync.dma_start(out=out_words[:, g * GROUP : (g + 1) * GROUP], in_=out_codes[g][:])
 
         pieces = [slice(sum(WIDTHS[:k]), sum(WIDTHS[: k + 1])) for k in range(len(WIDTHS))]
+        for cols in pieces[:2]:
+            round_into_pairs(PACK - 1, cols, nc.vector.tensor_copy)
         ahead = interleave(pieces[0])
         for k, cols in enumerate(pieces):
             current = ahead

@@ -67,11 +67,11 @@ def tile_list_msg_silu_noneP_kernel(
         w_raw = [keep.tile([P, R], I32, name="ws_raw"), keep.tile([P, R], I32, name="wt_raw")]
         nc.sync.dma_start(out=w_raw[SOURCE][:], in_=words_of(ws_words))
         load_scale_rows(tab_plane, 0, tab_scales, range(QUADS))
-        load_scale_rows(w_plane, 4 * SOURCE, ws_scales, range(2))
+        nc.sync.dma_start(out=w_raw[TARGET][:], in_=words_of(wt_words))
+        load_scale_rows(w_plane, 4 * SOURCE, ws_scales, range(1))
         tab_sb = keep.tile([P, T], I32, name="tab_sb", align_bytes=64)
         nc.sync.dma_start(out=tab_sb[:], in_=words_of(tab_words))
-        nc.sync.dma_start(out=w_raw[TARGET][:], in_=words_of(wt_words))
-        load_scale_rows(w_plane, 4 * SOURCE, ws_scales, range(2, QUADS))
+        load_scale_rows(w_plane, 4 * SOURCE, ws_scales, range(1, QUADS))
         load_scale_rows(w_plane, 4 * TARGET, wt_scales, range(QUADS))
         sm_sb = keep.tile([P, PACK, 8], F32, name="sm_sb")
         wd_raw = keep.tile([P, PACK, N], F32, name="wd_raw")
@@ -96,24 +96,27 @@ def tile_list_msg_silu_noneP_kernel(
 
         picked_words, picked_scales = {}, {}
 
-        def gather(window, dtype, picked, looks, count, tag):
-            got = keep.tile([P, len(looks), count * EDGES], dtype, name="picked_" + tag, tag=tag, align_bytes=64)
-            for u, (chunk, end) in enumerate(looks):
-                nc.vector.tensor_copy(got[:, u, :], window.indirect(entries(end, edges_of(chunk, count))))
-                for c in range(count):
-                    picked[chunk + c, end] = got[:, u, edges_of(c)]
+        def gather(window, dtype, picked, looks, tag):
+            total = sum(len(chunks) for end, chunks in looks)
+            got = keep.tile([P, total * EDGES], dtype, name="picked_" + tag, tag=tag, align_bytes=64)
+            place = 0
+            for end, chunks in looks:
+                source = window.indirect(entries(end, edges_of(chunks.start, len(chunks))))
+                nc.vector.tensor_copy(got[:, edges_of(place, len(chunks))], source)
+                for chunk in chunks:
+                    picked[chunk, end] = got[:, edges_of(place)]
+                    place = place + 1
 
-        def gather_words(looks, count, tag):
-            gather(tab_sb[:].bitcast(U32), U32, picked_words, looks, count, tag)
+        def gather_words(looks, tag):
+            gather(tab_sb[:].bitcast(U32), U32, picked_words, looks, tag)
 
-        def gather_scales(looks, count, tag):
-            gather(tab_plane[:], U8, picked_scales, looks, count, tag)
+        def gather_scales(looks, tag):
+            gather(tab_plane[:], U8, picked_scales, looks, tag)
 
         w_codes = keep.tile([P, 2, PACK, P], I32, name="w_codes", align_bytes=64)
         w_scales = keep.tile([P, PACK, P], U8, name="w_scales", align_bytes=64)
         wd_codes = keep.tile([P, PACK, P], U32, name="wd_codes", align_bytes=64)
         wd_scales = keep.tile([P, PACK, P], U8, name="wd_scales", align_bytes=64)
-        h_codes = keep.tile([P, J], U32, name="h_codes", align_bytes=64)
         h_scales = keep.tile([P, J], U8, name="h_scales", align_bytes=64)
 
         def sums(chunk, slices, bank_name):
@@ -132,12 +135,12 @@ def tile_list_msg_silu_noneP_kernel(
             return bank
 
         def activate_first():
-            act = keep.tile([P, PACK, EDGES], F32, name="act", tag="behind_act", align_bytes=64)
             h_pairs = keep.tile([P, 2, EDGES * 2], BF16, name="h_pairs", tag="behind_h_rows0", align_bytes=64)
             for t in range(PACK):
-                nc.scalar.activation(act[:, t : t + 1, :], sums(0, [t], "a_bank%d" % (t % 2))[:], SILU)
-                nc.scalar.activation(h_pairs[:, t // 2, t % 2 :: 2], act[:, t, :], COPY, scale=sm_sb[:, t, 0:1])
-            grouped = keep.tile([P, EDGES * PACK], BF16, name="h_grouped0", align_bytes=64)
+                act = keep.tile([P, 1, EDGES], F32, name="act", tag=("first_act", "behind_act")[t % 2], align_bytes=64)
+                nc.scalar.activation(act[:], sums(0, [t], "a_bank%d" % (t % 2))[:], SILU)
+                nc.scalar.activation(h_pairs[:, t // 2, t % 2 :: 2], act[:, 0, :], COPY, scale=sm_sb[:, t, 0:1])
+            grouped = keep.tile([P, EDGES * PACK], BF16, name="h_grouped0", tag="behind_h0", align_bytes=64)
             nc.scalar.copy(
                 out=grouped[:].bitcast(U32).rearrange("p (e u) -> p e u", u=2),
                 in_=h_pairs[:].rearrange("p u x -> p (u x)").bitcast(U32).rearrange("p (u e) -> p e u", u=2),
@@ -197,28 +200,35 @@ def tile_list_msg_silu_noneP_kernel(
             )
 
         deal_words(SOURCE)
-        gather_scales([(0, SOURCE), (0, TARGET)], 2, "first_scales")
-        gather_scales([(2, SOURCE)], 1, "third_source_scales")
-        gather_words([(0, SOURCE), (0, TARGET)], 1, "behind_first_sums")
+        gather_scales([(SOURCE, range(0, 2)), (TARGET, range(0, 2))], "first_scales")
         deal_words(TARGET)
+        gather_scales([(SOURCE, range(2, 4))], "later_source_scales")
+        gather_words([(SOURCE, range(0, 1)), (TARGET, range(0, 1))], "first_words")
         nc.vector.tensor_copy(
             out=w_scales[:].rearrange("p t m -> p (t m)").bitcast(I32).rearrange("p (t b c) -> p t b c", t=PACK, c=RUN // 4),
             in_=w_plane[:].bitcast(I32).rearrange("p (b t c) -> p t b c", t=PACK, c=RUN // 4),
         )
 
-        gather_words([(1, SOURCE), (1, TARGET)], 3, "behind_w_scales")
-        wd_grouped = keep.tile([P, PACK, P, PACK], BF16, name="wd_grouped", align_bytes=64)
-        nc.vector.tensor_copy(
-            out=wd_grouped[:].rearrange("p i m t -> p m t i"), in_=wd_raw[:].rearrange("p t (m i) -> p m t i", i=PACK)
-        )
-        nc.vector.quantize_mx(
-            out=wd_codes[:].rearrange("p i m -> p (i m)").bitcast(FP8X4),
-            scales=wd_scales[:].rearrange("p i m -> p (i m)"),
-            in_=wd_grouped[:].rearrange("p i m t -> p (i m t)"),
-        )
+        gather_words([(TARGET, range(1, 3)), (SOURCE, range(1, 4))], "behind_w_scales")
+        wd_grouped = [
+            keep.tile([P, 2, P, PACK], BF16, name="wd_grouped%d" % u, tag="behind_wd%d" % u, align_bytes=64) for u in range(2)
+        ]
+        for u in range(2):
+            nc.vector.tensor_copy(
+                out=wd_grouped[u][:].rearrange("p i m t -> p m t i"),
+                in_=wd_raw[:].rearrange("p t (m i) -> p m t i", i=PACK)[:, :, :, 2 * u : 2 * u + 2],
+            )
+        for u in range(2):
+            nc.vector.quantize_mx(
+                out=wd_codes[:, 2 * u : 2 * u + 2, :].rearrange("p i m -> p (i m)").bitcast(FP8X4),
+                scales=wd_scales[:, 2 * u : 2 * u + 2, :].rearrange("p i m -> p (i m)"),
+                in_=wd_grouped[u][:].rearrange("p i m t -> p (i m t)"),
+            )
+        h_codes = keep.tile([P, J], U32, name="h_codes", tag="behind_wd0", align_bytes=64)
 
         quantise_h(0, activate_first())
-        gather_scales([(2, TARGET), (3, SOURCE), (3, TARGET)], 1, "behind_h_rows0")
+        gather_words([(TARGET, range(3, 4))], "behind_h_rows0")
+        gather_scales([(TARGET, range(2, 4))], "behind_h0")
         pages.append(keep.tile([P, T], F32, name="page2", tag="behind_gathers", align_bytes=64))
         nc.gpsimd.memset(pages[2][:].bitcast(I32), 0)
         pages.append(pages[0])

@@ -61,32 +61,22 @@ def tile_list_msg_silu_noneP_kernel(
         nc.vector.memset(tab_plane[:].bitcast(I32), 0)
         nc.vector.memset(w_plane[:].bitcast(I32), 0)
 
+        sm_sb = keep.tile([P, PACK], F32, name="sm_sb")
+        nc.sync.dma_start(out=sm_sb[:], in_=sm.rearrange("(p t) -> p t", t=PACK))
         lists = [keep.tile([P, J // PER_COLUMN], U16, name="list%d" % end) for end in (SOURCE, TARGET)]
         nc.sync.dma_start(lists[SOURCE][:], offs)
         nc.sync.dma_start(lists[TARGET][:], offs2)
         w_raw = [keep.tile([P, R], I32, name="ws_raw"), keep.tile([P, R], I32, name="wt_raw")]
         nc.sync.dma_start(out=w_raw[SOURCE][:], in_=words_of(ws_words))
         load_scale_rows(tab_plane, 0, tab_scales, range(QUADS))
-        nc.sync.dma_start(out=w_raw[TARGET][:], in_=words_of(wt_words))
-        load_scale_rows(w_plane, 4 * SOURCE, ws_scales, range(1))
+        load_scale_rows(w_plane, 4 * SOURCE, ws_scales, range(2))
         tab_sb = keep.tile([P, T], I32, name="tab_sb", align_bytes=64)
         nc.sync.dma_start(out=tab_sb[:], in_=words_of(tab_words))
-        load_scale_rows(w_plane, 4 * SOURCE, ws_scales, range(1, QUADS))
+        nc.sync.dma_start(out=w_raw[TARGET][:], in_=words_of(wt_words))
+        load_scale_rows(w_plane, 4 * SOURCE, ws_scales, range(2, QUADS))
         load_scale_rows(w_plane, 4 * TARGET, wt_scales, range(QUADS))
-        sm_sb = keep.tile([P, PACK, 8], F32, name="sm_sb")
         wd_raw = keep.tile([P, PACK, N], F32, name="wd_raw")
-
-        def load_wd(slices):
-            for t in slices:
-                nc.sync.dma_start(out=wd_raw[:, t, :], in_=wd.rearrange("(b t c) n -> t b c n", t=PACK, c=RUN)[t])
-
-        load_wd(range(2))
-        with nc.allow_non_contiguous_dma(reason="one factor for each partition"):
-            for t in range(PACK):
-                nc.sync.dma_start(
-                    out=sm_sb[:, t, 0:1], in_=sm.rearrange("(b t c o) -> t b c o", t=PACK, c=RUN, o=1)[t]
-                )
-        load_wd(range(2, PACK))
+        nc.sync.dma_start(out=wd_raw[:], in_=wd.rearrange("(p t) n -> p t n", t=PACK))
         wgo_sb = keep.tile([P, J], F32, name="wgo_sb", align_bytes=64)
         nc.sync.dma_start(out=wgo_sb[:], in_=wgo)
 
@@ -139,8 +129,8 @@ def tile_list_msg_silu_noneP_kernel(
             for t in range(PACK):
                 act = keep.tile([P, 1, EDGES], F32, name="act", tag=("first_act", "behind_act")[t % 2], align_bytes=64)
                 nc.scalar.activation(act[:], sums(0, [t], "a_bank%d" % (t % 2))[:], SILU)
-                nc.scalar.activation(h_pairs[:, t // 2, t % 2 :: 2], act[:, 0, :], COPY, scale=sm_sb[:, t, 0:1])
-            grouped = keep.tile([P, EDGES * PACK], BF16, name="h_grouped0", tag="behind_h0", align_bytes=64)
+                nc.scalar.activation(h_pairs[:, t // 2, t % 2 :: 2], act[:, 0, :], COPY, scale=sm_sb[:, t : t + 1])
+            grouped = keep.tile([P, EDGES * PACK], BF16, name="h_grouped0", align_bytes=64)
             nc.scalar.copy(
                 out=grouped[:].bitcast(U32).rearrange("p (e u) -> p e u", u=2),
                 in_=h_pairs[:].rearrange("p u x -> p (u x)").bitcast(U32).rearrange("p (u e) -> p e u", u=2),
@@ -153,7 +143,7 @@ def tile_list_msg_silu_noneP_kernel(
                 nc.scalar.activation(act[:, low : low + 2, :], sums(chunk, [low, low + 1], "a_bank%d" % (low // 2))[:], SILU)
             h_rows = keep.tile([P, PACK, EDGES], BF16, name="h_rows", tag="behind_h_rows%d" % chunk, align_bytes=64)
             for t in range(PACK):
-                nc.scalar.activation(h_rows[:, t, :], act[:, t, :], COPY, scale=sm_sb[:, t, 0:1])
+                nc.scalar.activation(h_rows[:, t, :], act[:, t, :], COPY, scale=sm_sb[:, t : t + 1])
             return h_rows
 
         def group_rows(chunk, h_rows):
@@ -195,21 +185,17 @@ def tile_list_msg_silu_noneP_kernel(
 
         def deal_words(end):
             nc.vector.tensor_copy(
-                out=w_codes[:, end].rearrange("p t (b c) -> p t b c", c=RUN),
-                in_=w_raw[end][:].rearrange("p (b t c) -> p t b c", t=PACK, c=RUN),
+                out=w_codes[:, end].rearrange("p t m -> p m t"), in_=w_raw[end][:].rearrange("p (m t) -> p m t", t=PACK)
             )
 
         deal_words(SOURCE)
         gather_scales([(SOURCE, range(0, 2)), (TARGET, range(0, 2))], "first_scales")
+        gather_words([(SOURCE, range(0, 1)), (TARGET, range(0, 1))], "behind_first_sums")
         deal_words(TARGET)
-        gather_scales([(SOURCE, range(2, 4))], "later_source_scales")
-        gather_words([(SOURCE, range(0, 1)), (TARGET, range(0, 1))], "first_words")
-        nc.vector.tensor_copy(
-            out=w_scales[:].rearrange("p t m -> p (t m)").bitcast(I32).rearrange("p (t b c) -> p t b c", t=PACK, c=RUN // 4),
-            in_=w_plane[:].bitcast(I32).rearrange("p (b t c) -> p t b c", t=PACK, c=RUN // 4),
-        )
+        nc.vector.tensor_copy(out=w_scales[:], in_=w_plane[:].rearrange("p (m t) -> p t m", t=PACK))
 
-        gather_words([(TARGET, range(1, 3)), (SOURCE, range(1, 4))], "behind_w_scales")
+        gather_words([(SOURCE, range(1, 4)), (TARGET, range(1, 4))], "behind_w_scales")
+        gather_scales([(SOURCE, range(2, 3))], "behind_first_sums")
         wd_grouped = [
             keep.tile([P, 2, P, PACK], BF16, name="wd_grouped%d" % u, tag="behind_wd%d" % u, align_bytes=64) for u in range(2)
         ]
@@ -227,8 +213,7 @@ def tile_list_msg_silu_noneP_kernel(
         h_codes = keep.tile([P, J], U32, name="h_codes", tag="behind_wd0", align_bytes=64)
 
         quantise_h(0, activate_first())
-        gather_words([(TARGET, range(3, 4))], "behind_h_rows0")
-        gather_scales([(TARGET, range(2, 4))], "behind_h0")
+        gather_scales([(TARGET, range(2, 4)), (SOURCE, range(3, 4))], "behind_h_rows0")
         pages.append(keep.tile([P, T], F32, name="page2", tag="behind_gathers", align_bytes=64))
         nc.gpsimd.memset(pages[2][:].bitcast(I32), 0)
         pages.append(pages[0])

@@ -72,9 +72,11 @@ def tile_list_msg_silu_noneP_kernel(
         load_scale_rows(w_plane, 4 * SOURCE, ws_scales, range(2))
         tab_sb = keep.tile([P, T], I32, name="tab_sb", align_bytes=64)
         nc.sync.dma_start(out=tab_sb[:], in_=words_of(tab_words))
-        nc.sync.dma_start(out=w_raw[TARGET][:], in_=words_of(wt_words))
         load_scale_rows(w_plane, 4 * SOURCE, ws_scales, range(2, QUADS))
         load_scale_rows(w_plane, 4 * TARGET, wt_scales, range(QUADS))
+        nc.sync.dma_start(out=w_raw[TARGET][:], in_=words_of(wt_words))
+        warm = keep.tile([P, 1], F32, name="warm")
+        nc.scalar.activation(warm[:], sm_sb[:, 0:1], SILU)
         wd_raw = keep.tile([P, PACK, N], F32, name="wd_raw")
         nc.sync.dma_start(out=wd_raw[:], in_=wd.rearrange("(p t) n -> p t n", t=PACK))
         wgo_sb = keep.tile([P, J], F32, name="wgo_sb", align_bytes=64)
@@ -184,17 +186,18 @@ def tile_list_msg_silu_noneP_kernel(
             scatter(i, edges, messages(i, edges, bank_name, tag))
 
         def deal_words(end):
-            nc.vector.tensor_copy(
-                out=w_codes[:, end].rearrange("p t m -> p m t"), in_=w_raw[end][:].rearrange("p (m t) -> p m t", t=PACK)
+            nc.scalar.copy(
+                out=w_codes[:, end].bitcast(U32).rearrange("p t m -> p m t"),
+                in_=w_raw[end][:].bitcast(U32).rearrange("p (m t) -> p m t", t=PACK),
             )
 
         deal_words(SOURCE)
         gather_scales([(SOURCE, range(0, 2)), (TARGET, range(0, 2))], "first_scales")
-        gather_words([(SOURCE, range(0, 1)), (TARGET, range(0, 1))], "behind_first_sums")
+        gather_words([(SOURCE, range(0, 1))], "behind_first_sums")
         deal_words(TARGET)
         nc.vector.tensor_copy(out=w_scales[:], in_=w_plane[:].rearrange("p (m t) -> p t m", t=PACK))
 
-        gather_words([(SOURCE, range(1, 4)), (TARGET, range(1, 4))], "behind_w_scales")
+        gather_words([(TARGET, range(0, 1)), (SOURCE, range(1, 4)), (TARGET, range(1, 4))], "behind_w_scales")
         gather_scales([(SOURCE, range(2, 3))], "behind_first_sums")
         wd_grouped = [
             keep.tile([P, 2, P, PACK], BF16, name="wd_grouped%d" % u, tag="behind_wd%d" % u, align_bytes=64) for u in range(2)

@@ -38,6 +38,20 @@ def tile_list_msg_silu_noneP_kernel(
     nc = tc.nc
     with ExitStack() as ctx:
         keep = ctx.enter_context(tc.tile_pool(name="keep", bufs=1))
+        placed = ctx.enter_context(tc.tile_pool(name="placed", bufs=1))
+        offsets = {}
+        for chunk in (1, 2):
+            base = (chunk - 1) * 6144
+            offsets["h_rows%d" % chunk] = base + 512
+            offsets["second%d" % chunk] = base
+            offsets["third%d" % chunk] = base + 1024
+            offsets["act%d" % (chunk + 1)] = base + 2048
+
+        def tile(shape, dtype, name, tag):
+            if tag in offsets:
+                return placed.tile(shape, dtype, name=name, tag=tag, align_bytes=64, offset=offsets[tag])
+            return keep.tile(shape, dtype, name=name, tag=tag, align_bytes=64)
+
         psum = ctx.enter_context(tc.psum_pool(name="psum", bufs=2))
 
         def load_scale_rows(plane, shift, rows, quads):
@@ -56,7 +70,7 @@ def tile_list_msg_silu_noneP_kernel(
         def entries(end, edges):
             return lists[end][:, edges.start // PER_COLUMN : edges.stop // PER_COLUMN]
 
-        tab_plane = keep.tile([P, T], U8, name="tab_plane", tag="behind_gathers", align_bytes=64)
+        tab_plane = keep.tile([P, T], U8, name="tab_plane", align_bytes=64)
         w_plane = keep.tile([P, R], U8, name="w_plane", tag="behind_w_scales", align_bytes=64)
         nc.vector.memset(tab_plane[:].bitcast(I32), 0)
         nc.vector.memset(w_plane[:].bitcast(I32), 0)
@@ -67,8 +81,8 @@ def tile_list_msg_silu_noneP_kernel(
         nc.sync.dma_start(lists[SOURCE][:], offs)
         nc.sync.dma_start(lists[TARGET][:], offs2)
         w_raw = [keep.tile([P, R], I32, name="ws_raw"), keep.tile([P, R], I32, name="wt_raw")]
-        nc.sync.dma_start(out=w_raw[SOURCE][:], in_=words_of(ws_words))
         load_scale_rows(tab_plane, 0, tab_scales, range(QUADS))
+        nc.sync.dma_start(out=w_raw[SOURCE][:], in_=words_of(ws_words))
         load_scale_rows(w_plane, 4 * SOURCE, ws_scales, range(2))
         tab_sb = keep.tile([P, T], I32, name="tab_sb", align_bytes=64)
         nc.sync.dma_start(out=tab_sb[:], in_=words_of(tab_words))
@@ -129,27 +143,34 @@ def tile_list_msg_silu_noneP_kernel(
         def activate_first():
             h_pairs = keep.tile([P, 2, EDGES * 2], BF16, name="h_pairs", tag="behind_h_rows0", align_bytes=64)
             for t in range(PACK):
-                act = keep.tile([P, 1, EDGES], F32, name="act", tag=("first_act", "behind_act")[t % 2], align_bytes=64)
+                act = keep.tile([P, 1, EDGES], F32, name="act", tag=("act1_1", "act1_0")[t % 2], align_bytes=64)
                 nc.scalar.activation(act[:], sums(0, [t], "a_bank%d" % (t % 2))[:], SILU)
                 nc.scalar.activation(h_pairs[:, t // 2, t % 2 :: 2], act[:, 0, :], COPY, scale=sm_sb[:, t : t + 1])
-            grouped = keep.tile([P, EDGES * PACK], BF16, name="h_grouped0", align_bytes=64)
-            nc.scalar.copy(
-                out=grouped[:].bitcast(U32).rearrange("p (e u) -> p e u", u=2),
-                in_=h_pairs[:].rearrange("p u x -> p (u x)").bitcast(U32).rearrange("p (u e) -> p e u", u=2),
+            grouped = keep.tile([P, EDGES * PACK], BF16, name="h_grouped0", tag="behind_h0", align_bytes=64)
+            nc.vector.tensor_copy(
+                out=grouped[:].bitcast(I32).rearrange("p (e u) -> p e u", u=2),
+                in_=h_pairs[:].rearrange("p u x -> p (u x)").bitcast(I32).rearrange("p (u e) -> p e u", u=2),
             )
             return grouped
 
-        def activate(chunk):
-            act = keep.tile([P, PACK, EDGES], F32, name="act", tag="behind_act", align_bytes=64)
+        def silu_rows(chunk):
+            if chunk == 1:
+                acts = [tile([P, 2, EDGES], F32, "act", "act1_%d" % half)[:] for half in range(2)]
+            else:
+                act = tile([P, PACK, EDGES], F32, "act", "act%d" % chunk)
+                acts = [act[:, 0:2, :], act[:, 2:4, :]]
             for low in (0, 2):
-                nc.scalar.activation(act[:, low : low + 2, :], sums(chunk, [low, low + 1], "a_bank%d" % (low // 2))[:], SILU)
-            h_rows = keep.tile([P, PACK, EDGES], BF16, name="h_rows", tag="behind_h_rows%d" % chunk, align_bytes=64)
+                nc.scalar.activation(acts[low // 2], sums(chunk, [low, low + 1], "a_bank%d" % (low // 2))[:], SILU)
+            return acts
+
+        def scale_rows(chunk, act):
+            h_rows = tile([P, PACK, EDGES], BF16, "h_rows", "h_rows%d" % chunk)
             for t in range(PACK):
-                nc.scalar.activation(h_rows[:, t, :], act[:, t, :], COPY, scale=sm_sb[:, t : t + 1])
+                nc.scalar.activation(h_rows[:, t, :], act[t // 2][:, t % 2, :], COPY, scale=sm_sb[:, t : t + 1])
             return h_rows
 
         def group_rows(chunk, h_rows):
-            grouped = keep.tile([P, EDGES * PACK], BF16, name="h_grouped%d" % chunk, align_bytes=64)
+            grouped = keep.tile([P, EDGES * PACK], BF16, name="h_grouped", tag="behind_h%d" % chunk, align_bytes=64)
             nc.scalar.copy(
                 out=grouped[:].rearrange("p (e f t) -> p e t f", f=4, t=PACK),
                 in_=h_rows[:].rearrange("p t (e f) -> p e t f", f=4),
@@ -163,7 +184,7 @@ def tile_list_msg_silu_noneP_kernel(
 
         def messages(i, edges, bank_name, tag=None):
             name = "y%d_%d" % (i, edges.start)
-            y = keep.tile([P, edges.stop - edges.start], F32, name=name, tag=tag or name, align_bytes=64)
+            y = tile([P, edges.stop - edges.start], F32, name, tag or name)
             width = min(edges.stop - edges.start, BANK)
             for start in range(edges.start, edges.stop, width):
                 bank = psum.tile([P, width], F32, name=bank_name)
@@ -192,13 +213,12 @@ def tile_list_msg_silu_noneP_kernel(
             )
 
         deal_words(SOURCE)
-        gather_scales([(SOURCE, range(0, 2)), (TARGET, range(0, 2))], "first_scales")
+        gather_scales([(SOURCE, range(0, 4)), (TARGET, range(0, 2))], "first_scales")
         gather_words([(SOURCE, range(0, 1))], "behind_first_sums")
         deal_words(TARGET)
         nc.vector.tensor_copy(out=w_scales[:], in_=w_plane[:].rearrange("p (m t) -> p t m", t=PACK))
 
-        gather_words([(TARGET, range(0, 1)), (SOURCE, range(1, 4)), (TARGET, range(1, 4))], "behind_w_scales")
-        gather_scales([(SOURCE, range(2, 3))], "behind_first_sums")
+        gather_words([(TARGET, range(0, 1)), (SOURCE, range(1, 4)), (TARGET, range(1, 3))], "behind_w_scales")
         wd_grouped = [
             keep.tile([P, 2, P, PACK], BF16, name="wd_grouped%d" % u, tag="behind_wd%d" % u, align_bytes=64) for u in range(2)
         ]
@@ -216,22 +236,26 @@ def tile_list_msg_silu_noneP_kernel(
         h_codes = keep.tile([P, J], U32, name="h_codes", tag="behind_wd0", align_bytes=64)
 
         quantise_h(0, activate_first())
-        gather_scales([(TARGET, range(2, 4)), (SOURCE, range(3, 4))], "behind_h_rows0")
-        pages.append(keep.tile([P, T], F32, name="page2", tag="behind_gathers", align_bytes=64))
+        gather_words([(TARGET, range(3, 4))], "behind_h0")
+        gather_scales([(TARGET, range(2, 4))], "behind_h_rows0")
+        rows = scale_rows(1, silu_rows(1))
+        send(0, edges_of(0), "y_first", "act1_0")
+        quantise_h(1, group_rows(1, rows))
+        pages.append(keep.tile([P, T], F32, name="page2", tag="behind_h1", align_bytes=64))
         nc.gpsimd.memset(pages[2][:].bitcast(I32), 0)
         pages.append(pages[0])
-        send(0, edges_of(0), "y_first")
-        send(1, edges_of(0), "y_other")
-        quantise_h(1, group_rows(1, activate(1)))
-        send(2, edges_of(0), "y_other", "behind_h_rows1")
+        send(1, edges_of(0), "y_other", "second1")
+        third = messages(2, edges_of(0), "y_other", "third1")
+        act = silu_rows(2)
         send(0, edges_of(1), "y_first")
-        send(1, edges_of(1), "y_other")
-        quantise_h(2, group_rows(2, activate(2)))
-        send(2, edges_of(1), "y_other", "behind_h_rows2")
-        last_rows = activate(3)
-        send(0, edges_of(2), "y_first", "behind_act")
-        quantise_h(3, group_rows(3, last_rows))
-        send(1, edges_of(2), "y_other", "behind_h_rows3")
+        scatter(2, edges_of(0), third)
+        quantise_h(2, group_rows(2, scale_rows(2, act)))
+        send(1, edges_of(1), "y_other", "second2")
+        send(2, edges_of(1), "y_other", "third2")
+        rows = scale_rows(3, silu_rows(3))
+        send(0, edges_of(2), "y_first", "act3")
+        quantise_h(3, group_rows(3, rows))
+        send(1, edges_of(2), "y_other", "h_rows3")
         send(0, edges_of(3), "y_first")
         send(1, edges_of(3), "y_other")
         send(2, edges_of(2, 2), "a_bank0")

@@ -75,22 +75,20 @@ def tile_list_msg_silu_noneP_kernel(
         nc.vector.memset(tab_plane[:].bitcast(I32), 0)
         nc.vector.memset(w_plane[:].bitcast(I32), 0)
 
-        sm_sb = keep.tile([P, PACK], F32, name="sm_sb")
-        nc.sync.dma_start(out=sm_sb[:], in_=sm.rearrange("(p t) -> p t", t=PACK))
         lists = [keep.tile([P, J // PER_COLUMN], U16, name="list%d" % end) for end in (SOURCE, TARGET)]
         nc.sync.dma_start(lists[SOURCE][:], offs)
         nc.sync.dma_start(lists[TARGET][:], offs2)
-        w_raw = [keep.tile([P, R], I32, name="ws_raw"), keep.tile([P, R], I32, name="wt_raw")]
         load_scale_rows(tab_plane, 0, tab_scales, range(QUADS))
+        w_raw = [keep.tile([P, R], I32, name="ws_raw"), keep.tile([P, R], I32, name="wt_raw")]
         nc.sync.dma_start(out=w_raw[SOURCE][:], in_=words_of(ws_words))
-        load_scale_rows(w_plane, 4 * SOURCE, ws_scales, range(2))
+        nc.sync.dma_start(out=w_raw[TARGET][:], in_=words_of(wt_words))
+        load_scale_rows(w_plane, 4 * SOURCE, ws_scales, range(1))
         tab_sb = keep.tile([P, T], I32, name="tab_sb", align_bytes=64)
         nc.sync.dma_start(out=tab_sb[:], in_=words_of(tab_words))
-        load_scale_rows(w_plane, 4 * SOURCE, ws_scales, range(2, QUADS))
+        load_scale_rows(w_plane, 4 * SOURCE, ws_scales, range(1, QUADS))
         load_scale_rows(w_plane, 4 * TARGET, wt_scales, range(QUADS))
-        nc.sync.dma_start(out=w_raw[TARGET][:], in_=words_of(wt_words))
-        warm = keep.tile([P, 1], F32, name="warm")
-        nc.scalar.activation(warm[:], sm_sb[:, 0:1], SILU)
+        sm_sb = keep.tile([P, PACK], F32, name="sm_sb")
+        nc.sync.dma_start(out=sm_sb[:], in_=sm.rearrange("(p t) -> p t", t=PACK))
         wd_raw = keep.tile([P, PACK, N], F32, name="wd_raw")
         nc.sync.dma_start(out=wd_raw[:], in_=wd.rearrange("(p t) n -> p t n", t=PACK))
         wgo_sb = keep.tile([P, J], F32, name="wgo_sb", align_bytes=64)

@@ -39,13 +39,11 @@ def tile_list_msg_silu_noneP_kernel(
     with ExitStack() as ctx:
         keep = ctx.enter_context(tc.tile_pool(name="keep", bufs=1))
         placed = ctx.enter_context(tc.tile_pool(name="placed", bufs=1))
-        offsets = {}
-        for chunk in (1, 2):
-            base = (chunk - 1) * 6144
-            offsets["h_rows%d" % chunk] = base + 512
-            offsets["second%d" % chunk] = base
-            offsets["third%d" % chunk] = base + 1024
-            offsets["act%d" % (chunk + 1)] = base + 2048
+        offsets = {
+            "act1_1": 0, "act0_odd": 1536, "act1_0": 2048, "second0": 3072,
+            "act2_1": 4096, "h_rows1": 6080, "third0": 6144, "act2_0": 7680, "first1": 7680, "second1": 8704,
+            "third1": 10240, "h_rows2": 10752, "act3": 12288,
+        }
 
         def tile(shape, dtype, name, tag):
             if tag in offsets:
@@ -70,7 +68,7 @@ def tile_list_msg_silu_noneP_kernel(
         def entries(end, edges):
             return lists[end][:, edges.start // PER_COLUMN : edges.stop // PER_COLUMN]
 
-        tab_plane = keep.tile([P, T], U8, name="tab_plane", align_bytes=64)
+        tab_plane = keep.tile([P, T], U8, name="tab_plane", tag="behind_gathers", align_bytes=64)
         w_plane = keep.tile([P, R], U8, name="w_plane", tag="behind_w_scales", align_bytes=64)
         nc.vector.memset(tab_plane[:].bitcast(I32), 0)
         nc.vector.memset(w_plane[:].bitcast(I32), 0)
@@ -141,7 +139,7 @@ def tile_list_msg_silu_noneP_kernel(
         def activate_first():
             h_pairs = keep.tile([P, 2, EDGES * 2], BF16, name="h_pairs", tag="behind_h_rows0", align_bytes=64)
             for t in range(PACK):
-                act = keep.tile([P, 1, EDGES], F32, name="act", tag=("act1_1", "act1_0")[t % 2], align_bytes=64)
+                act = tile([P, 1, EDGES], F32, "act", ("act0_even", "act0_odd")[t % 2])
                 nc.scalar.activation(act[:], sums(0, [t], "a_bank%d" % (t % 2))[:], SILU)
                 nc.scalar.activation(h_pairs[:, t // 2, t % 2 :: 2], act[:, 0, :], COPY, scale=sm_sb[:, t : t + 1])
             grouped = keep.tile([P, EDGES * PACK], BF16, name="h_grouped0", tag="behind_h0", align_bytes=64)
@@ -152,8 +150,8 @@ def tile_list_msg_silu_noneP_kernel(
             return grouped
 
         def silu_rows(chunk):
-            if chunk == 1:
-                acts = [tile([P, 2, EDGES], F32, "act", "act1_%d" % half)[:] for half in range(2)]
+            if chunk < 3:
+                acts = [tile([P, 2, EDGES], F32, "act", "act%d_%d" % (chunk, half))[:] for half in range(2)]
             else:
                 act = tile([P, PACK, EDGES], F32, "act", "act%d" % chunk)
                 acts = [act[:, 0:2, :], act[:, 2:4, :]]
@@ -161,9 +159,10 @@ def tile_list_msg_silu_noneP_kernel(
                 nc.scalar.activation(acts[low // 2], sums(chunk, [low, low + 1], "a_bank%d" % (low // 2))[:], SILU)
             return acts
 
-        def scale_rows(chunk, act):
-            h_rows = tile([P, PACK, EDGES], BF16, "h_rows", "h_rows%d" % chunk)
-            for t in range(PACK):
+        def scale_rows(chunk, act, slices=range(PACK), h_rows=None):
+            if h_rows is None:
+                h_rows = tile([P, PACK, EDGES], BF16, "h_rows", "h_rows%d" % chunk)
+            for t in slices:
                 nc.scalar.activation(h_rows[:, t, :], act[t // 2][:, t % 2, :], COPY, scale=sm_sb[:, t : t + 1])
             return h_rows
 
@@ -236,20 +235,23 @@ def tile_list_msg_silu_noneP_kernel(
         quantise_h(0, activate_first())
         gather_words([(TARGET, range(3, 4))], "behind_h0")
         gather_scales([(TARGET, range(2, 4))], "behind_h_rows0")
-        rows = scale_rows(1, silu_rows(1))
-        send(0, edges_of(0), "y_first", "act1_0")
-        quantise_h(1, group_rows(1, rows))
-        pages.append(keep.tile([P, T], F32, name="page2", tag="behind_h1", align_bytes=64))
+        pages.append(keep.tile([P, T], F32, name="page2", tag="behind_gathers", align_bytes=64))
         nc.gpsimd.memset(pages[2][:].bitcast(I32), 0)
         pages.append(pages[0])
-        send(1, edges_of(0), "y_other", "second1")
-        third = messages(2, edges_of(0), "y_other", "third1")
+        act = silu_rows(1)
+        send(0, edges_of(0), "y_first")
+        rows = scale_rows(1, act, range(2))
+        send(1, edges_of(0), "y_other", "second0")
+        scale_rows(1, act, range(2, PACK), rows)
+        quantise_h(1, group_rows(1, rows))
+        send(2, edges_of(0), "y_other", "third0")
         act = silu_rows(2)
-        send(0, edges_of(1), "y_first")
-        scatter(2, edges_of(0), third)
-        quantise_h(2, group_rows(2, scale_rows(2, act)))
-        send(1, edges_of(1), "y_other", "second2")
-        send(2, edges_of(1), "y_other", "third2")
+        rows = scale_rows(2, act, range(2))
+        send(0, edges_of(1), "y_first", "first1")
+        send(1, edges_of(1), "y_other", "second1")
+        scale_rows(2, act, range(2, PACK), rows)
+        quantise_h(2, group_rows(2, rows))
+        send(2, edges_of(1), "y_other", "third1")
         rows = scale_rows(3, silu_rows(3))
         send(0, edges_of(2), "y_first", "act3")
         quantise_h(3, group_rows(3, rows))

@@ -69,7 +69,7 @@ def tile_list_msg_silu_noneP_kernel(
             return lists[end][:, edges.start // PER_COLUMN : edges.stop // PER_COLUMN]
 
         tab_plane = keep.tile([P, T], U8, name="tab_plane", tag="behind_gathers", align_bytes=64)
-        w_plane = keep.tile([P, R], U8, name="w_plane", tag="behind_w_scales", align_bytes=64)
+        w_plane = keep.tile([P, R], U8, name="w_plane", align_bytes=64)
         nc.vector.memset(tab_plane[:].bitcast(I32), 0)
         nc.vector.memset(w_plane[:].bitcast(I32), 0)
 
@@ -213,9 +213,9 @@ def tile_list_msg_silu_noneP_kernel(
         gather_scales([(SOURCE, range(0, 4)), (TARGET, range(0, 2))], "first_scales")
         gather_words([(SOURCE, range(0, 1))], "behind_first_sums")
         deal_words(TARGET)
-        nc.vector.tensor_copy(out=w_scales[:], in_=w_plane[:].rearrange("p (m t) -> p t m", t=PACK))
+        nc.gpsimd.tensor_copy(out=w_scales[:], in_=w_plane[:].rearrange("p (m t) -> p t m", t=PACK))
 
-        gather_words([(TARGET, range(0, 1)), (SOURCE, range(1, 4)), (TARGET, range(1, 3))], "behind_w_scales")
+        gather_words([(TARGET, range(0, 1)), (SOURCE, range(1, 4)), (TARGET, range(1, 3))], "later_words")
         wd_grouped = [
             keep.tile([P, 2, P, PACK], BF16, name="wd_grouped%d" % u, tag="behind_wd%d" % u, align_bytes=64) for u in range(2)
         ]

@@ -40,7 +40,7 @@ def tile_list_msg_silu_noneP_kernel(
         keep = ctx.enter_context(tc.tile_pool(name="keep", bufs=1))
         placed = ctx.enter_context(tc.tile_pool(name="placed", bufs=1))
         offsets = {
-            "act1_1": 0, "act0_odd": 1536, "act1_0": 2048, "second0": 3072,
+            "act1_1": 0, "h_pairs": 1024, "act1_0": 2048, "second0": 3072,
             "act2_1": 4096, "h_rows1": 6080, "third0": 6144, "act2_0": 7680, "first1": 7680, "second1": 8704,
             "third1": 10240, "h_rows2": 10752, "act3": 12288,
         }
@@ -121,31 +121,43 @@ def tile_list_msg_silu_noneP_kernel(
         wd_scales = keep.tile([P, PACK, P], U8, name="wd_scales", align_bytes=64)
         h_scales = keep.tile([P, J], U8, name="h_scales", align_bytes=64)
 
+        def one_pass(out, chunk, t, end):
+            nc.tensor.matmul_mx(
+                out=out,
+                lhsT=w_codes[:, end, t, :].bitcast(FP8X4),
+                lhsT_scale=w_scales[4 * end :, t, :],
+                rhs=picked_words[chunk, end].bitcast(FP8X4),
+                rhs_scale=picked_scales[chunk, end],
+                start=(end == SOURCE),
+                stop=(end == TARGET),
+            )
+
         def sums(chunk, slices, bank_name):
             bank = psum.tile([P, len(slices), EDGES], F32, name=bank_name)
             for u, t in enumerate(slices):
                 for end in (SOURCE, TARGET):
-                    nc.tensor.matmul_mx(
-                        out=bank[:, u, :],
-                        lhsT=w_codes[:, end, t, :].bitcast(FP8X4),
-                        lhsT_scale=w_scales[4 * end :, t, :],
-                        rhs=picked_words[chunk, end].bitcast(FP8X4),
-                        rhs_scale=picked_scales[chunk, end],
-                        start=(end == SOURCE),
-                        stop=(end == TARGET),
-                    )
+                    one_pass(bank[:, u, :], chunk, t, end)
             return bank
 
         def activate_first():
-            h_pairs = keep.tile([P, 2, EDGES * 2], BF16, name="h_pairs", tag="behind_h_rows0", align_bytes=64)
-            for t in range(PACK):
-                act = tile([P, 1, EDGES], F32, "act", ("act0_even", "act0_odd")[t % 2])
-                nc.scalar.activation(act[:], sums(0, [t], "a_bank%d" % (t % 2))[:], SILU)
-                nc.scalar.activation(h_pairs[:, t // 2, t % 2 :: 2], act[:, 0, :], COPY, scale=sm_sb[:, t : t + 1])
+            h_pairs = tile([P, 2, EDGES * 2], BF16, "h_pairs", "h_pairs")
+            banks = [psum.tile([P, EDGES], F32, name="a_bank%d" % (t % 2)) for t in range(PACK)]
+            for t, end in [(0, SOURCE), (1, SOURCE), (0, TARGET), (1, TARGET)]:
+                one_pass(banks[t][:], 0, t, end)
+            for t in (2, 3):
+                for end in (SOURCE, TARGET):
+                    one_pass(banks[t][:], 0, t, end)
+            acts = [tile([P, EDGES], F32, "act", tag) for tag in ("act0_0", "act0_1", "act0_2", "act0_3")]
+            for t in range(PACK + 1):
+                if t < PACK:
+                    nc.scalar.activation(acts[t][:], banks[t][:], SILU)
+                if t > 0:
+                    s = t - 1
+                    nc.scalar.activation(h_pairs[:, s // 2, s % 2 :: 2], acts[s][:], COPY, scale=sm_sb[:, s : s + 1])
             grouped = keep.tile([P, EDGES * PACK], BF16, name="h_grouped0", tag="behind_h0", align_bytes=64)
-            nc.vector.tensor_copy(
-                out=grouped[:].bitcast(I32).rearrange("p (e u) -> p e u", u=2),
-                in_=h_pairs[:].rearrange("p u x -> p (u x)").bitcast(I32).rearrange("p (u e) -> p e u", u=2),
+            nc.scalar.copy(
+                out=grouped[:].bitcast(U32).rearrange("p (e u) -> p e u", u=2),
+                in_=h_pairs[:].rearrange("p u x -> p (u x)").bitcast(U32).rearrange("p (u e) -> p e u", u=2),
             )
             return grouped
 
@@ -234,7 +246,7 @@ def tile_list_msg_silu_noneP_kernel(
 
         quantise_h(0, activate_first())
         gather_words([(TARGET, range(3, 4))], "behind_h0")
-        gather_scales([(TARGET, range(2, 4))], "behind_h_rows0")
+        gather_scales([(TARGET, range(2, 4))], "behind_wd1")
         pages.append(keep.tile([P, T], F32, name="page2", tag="behind_gathers", align_bytes=64))
         nc.gpsimd.memset(pages[2][:].bitcast(I32), 0)
         pages.append(pages[0])

@@ -116,7 +116,7 @@ def tile_list_msg_silu_noneP_kernel(
             gather(tab_plane[:], U8, picked_scales, looks, tag)
 
         w_codes = keep.tile([P, 2, PACK, P], I32, name="w_codes", align_bytes=64)
-        w_scales = keep.tile([P, PACK, P], U8, name="w_scales", align_bytes=64)
+        w_scales = [keep.tile([P, 2, P], U8, name="w_scales%d" % half, align_bytes=64) for half in range(2)]
         wd_codes = keep.tile([P, PACK, P], U32, name="wd_codes", align_bytes=64)
         wd_scales = keep.tile([P, PACK, P], U8, name="wd_scales", align_bytes=64)
         h_scales = keep.tile([P, J], U8, name="h_scales", align_bytes=64)
@@ -125,7 +125,7 @@ def tile_list_msg_silu_noneP_kernel(
             nc.tensor.matmul_mx(
                 out=out,
                 lhsT=w_codes[:, end, t, :].bitcast(FP8X4),
-                lhsT_scale=w_scales[4 * end :, t, :],
+                lhsT_scale=w_scales[t // 2][4 * end :, t % 2, :],
                 rhs=picked_words[chunk, end].bitcast(FP8X4),
                 rhs_scale=picked_scales[chunk, end],
                 start=(end == SOURCE),
@@ -225,7 +225,9 @@ def tile_list_msg_silu_noneP_kernel(
         gather_scales([(SOURCE, range(0, 4)), (TARGET, range(0, 2))], "first_scales")
         gather_words([(SOURCE, range(0, 1))], "behind_first_sums")
         deal_words(TARGET)
-        nc.gpsimd.tensor_copy(out=w_scales[:], in_=w_plane[:].rearrange("p (m t) -> p t m", t=PACK))
+        for half in range(2):
+            slices = w_plane[:].rearrange("p (m t) -> p t m", t=PACK)[:, 2 * half : 2 * half + 2, :]
+            nc.gpsimd.tensor_copy(out=w_scales[half][:], in_=slices)
 
         gather_words([(TARGET, range(0, 1)), (SOURCE, range(1, 4)), (TARGET, range(1, 3))], "later_words")
         wd_grouped = [

from contextlib import ExitStack

import concourse.mybir as mybir

K, R, N, T, J = 512, 512, 512, 2048, 1024
FLOPS = 2 * J * (2 * K * R + R * N)

F32 = mybir.dt.float32
BF16 = mybir.dt.bfloat16
I32 = mybir.dt.int32
U32 = mybir.dt.uint32
U16 = mybir.dt.uint16
U8 = mybir.dt.uint8
FP8X4 = mybir.dt.float8_e4m3fn_x4
SILU = mybir.ActivationFunctionType.Silu
COPY = mybir.ActivationFunctionType.Copy
MULT = mybir.AluOpType.mult

P = 128
PACK = 4
RUN = 8
QUADS = 4
BANK = 512
EDGES = 256
PER_COLUMN = 16
SOURCE, TARGET = 0, 1
GROUP = 512
BLOCK = 128
WIDTHS = [128, 128, 256, 256, 256, 256, 256, 256, 128, 128]
SCALAR_COLUMNS = 512
VECTOR_COLUMNS = 256
TURNS = [2, 0, 1, 3]


def tile_list_msg_silu_noneP_kernel(
    tc, tab_words, tab_scales, ws_words, ws_scales, wt_words, wt_scales, sm, wd, wgo, offs, offs2, out_0, out_1, out_2
):
    nc = tc.nc
    with ExitStack() as ctx:
        keep = ctx.enter_context(tc.tile_pool(name="keep", bufs=1))
        placed = ctx.enter_context(tc.tile_pool(name="placed", bufs=1))
        offsets = {
            "act1_1": 0, "h_pairs": 1024, "act1_0": 2048, "second0": 3072,
            "act2_1": 4096, "h_rows1": 6080, "third0": 6144, "act2_0": 7680, "first1": 7680, "second1": 8704,
            "third1": 10240, "h_rows2": 10752, "act3": 12288,
        }

        def tile(shape, dtype, name, tag):
            if tag in offsets:
                return placed.tile(shape, dtype, name=name, tag=tag, align_bytes=64, offset=offsets[tag])
            return keep.tile(shape, dtype, name=name, tag=tag, align_bytes=64)

        psum = ctx.enter_context(tc.psum_pool(name="psum", bufs=2))

        def load_scale_rows(plane, shift, rows, quads):
            for quad in quads:
                nc.sync.dma_start(
                    out=plane[32 * quad + shift : 32 * quad + shift + 4, :].bitcast(I32),
                    in_=rows[0, 4 * quad : 4 * quad + 4, :].bitcast(I32),
                )

        def words_of(packed):
            return packed[0].rearrange("p c i -> p (c i)").bitcast(I32)

        def edges_of(chunk, count=1):
            return slice(chunk * EDGES, (chunk + count) * EDGES)

        def entries(end, edges):
            return lists[end][:, edges.start // PER_COLUMN : edges.stop // PER_COLUMN]

        tab_plane = keep.tile([P, T], U8, name="tab_plane", tag="behind_gathers", align_bytes=64)
        w_plane = keep.tile([P, R], U8, name="w_plane", align_bytes=64)
        nc.vector.memset(tab_plane[:].bitcast(I32), 0)
        nc.vector.memset(w_plane[:].bitcast(I32), 0)

        lists = [keep.tile([P, J // PER_COLUMN], U16, name="list%d" % end) for end in (SOURCE, TARGET)]
        nc.sync.dma_start(lists[SOURCE][:], offs)
        nc.sync.dma_start(lists[TARGET][:], offs2)
        load_scale_rows(tab_plane, 0, tab_scales, range(QUADS))
        w_raw = [keep.tile([P, R], I32, name="ws_raw"), keep.tile([P, R], I32, name="wt_raw")]
        nc.sync.dma_start(out=w_raw[SOURCE][:], in_=words_of(ws_words))
        nc.sync.dma_start(out=w_raw[TARGET][:], in_=words_of(wt_words))
        load_scale_rows(w_plane, 4 * SOURCE, ws_scales, range(1))
        tab_sb = keep.tile([P, T], I32, name="tab_sb", align_bytes=64)
        nc.sync.dma_start(out=tab_sb[:], in_=words_of(tab_words))
        load_scale_rows(w_plane, 4 * SOURCE, ws_scales, range(1, QUADS))
        load_scale_rows(w_plane, 4 * TARGET, wt_scales, range(QUADS))
        sm_sb = keep.tile([P, PACK], F32, name="sm_sb")
        nc.sync.dma_start(out=sm_sb[:], in_=sm.rearrange("(p t) -> p t", t=PACK))
        wd_raw = keep.tile([P, PACK, N], F32, name="wd_raw")
        nc.sync.dma_start(out=wd_raw[:], in_=wd.rearrange("(p t) n -> p t n", t=PACK))
        wgo_sb = keep.tile([P, J], F32, name="wgo_sb", align_bytes=64)
        nc.sync.dma_start(out=wgo_sb[:], in_=wgo)

        pages = [keep.tile([P, T], F32, name="page%d" % i) for i in range(PACK - 2)]
        for page in pages:
            nc.vector.memset(page[:].bitcast(I32), 0)

        picked_words, picked_scales = {}, {}

        def gather(window, dtype, picked, looks, tag):
            total = sum(len(chunks) for end, chunks in looks)
            got = keep.tile([P, total * EDGES], dtype, name="picked_" + tag, tag=tag, align_bytes=64)
            place = 0
            for end, chunks in looks:
                source = window.indirect(entries(end, edges_of(chunks.start, len(chunks))))
                nc.vector.tensor_copy(got[:, edges_of(place, len(chunks))], source)
                for chunk in chunks:
                    picked[chunk, end] = got[:, edges_of(place)]
                    place = place + 1

        def gather_words(looks, tag):
            gather(tab_sb[:].bitcast(U32), U32, picked_words, looks, tag)

        def gather_scales(looks, tag):
            gather(tab_plane[:], U8, picked_scales, looks, tag)

        w_codes = keep.tile([P, 2, PACK, P], I32, name="w_codes", align_bytes=64)
        w_scales = [keep.tile([P, 2, P], U8, name="w_scales%d" % half, align_bytes=64) for half in range(2)]
        wd_codes = keep.tile([P, PACK, P], U32, name="wd_codes", align_bytes=64)
        wd_scales = keep.tile([P, PACK, P], U8, name="wd_scales", align_bytes=64)
        h_scales = keep.tile([P, J], U8, name="h_scales", align_bytes=64)

        def one_pass(out, chunk, t, end):
            nc.tensor.matmul_mx(
                out=out,
                lhsT=w_codes[:, end, t, :].bitcast(FP8X4),
                lhsT_scale=w_scales[t // 2][4 * end :, t % 2, :],
                rhs=picked_words[chunk, end].bitcast(FP8X4),
                rhs_scale=picked_scales[chunk, end],
                start=(end == SOURCE),
                stop=(end == TARGET),
            )

        def sums(chunk, slices, bank_name):
            bank = psum.tile([P, len(slices), EDGES], F32, name=bank_name)
            for u, t in enumerate(slices):
                for end in (SOURCE, TARGET):
                    one_pass(bank[:, u, :], chunk, t, end)
            return bank

        def activate_first():
            h_pairs = tile([P, 2, EDGES * 2], BF16, "h_pairs", "h_pairs")
            banks = [psum.tile([P, EDGES], F32, name="a_bank%d" % (t % 2)) for t in range(PACK)]
            for t, end in [(0, SOURCE), (1, SOURCE), (0, TARGET), (1, TARGET)]:
                one_pass(banks[t][:], 0, t, end)
            for t in (2, 3):
                for end in (SOURCE, TARGET):
                    one_pass(banks[t][:], 0, t, end)
            acts = [tile([P, EDGES], F32, "act", tag) for tag in ("act0_0", "act0_1", "act0_2", "act0_3")]
            for t in range(PACK + 1):
                if t < PACK:
                    nc.scalar.activation(acts[t][:], banks[t][:], SILU)
                if t > 0:
                    s = t - 1
                    nc.scalar.activation(h_pairs[:, s // 2, s % 2 :: 2], acts[s][:], COPY, scale=sm_sb[:, s : s + 1])
            grouped = keep.tile([P, EDGES * PACK], BF16, name="h_grouped0", tag="behind_h0", align_bytes=64)
            nc.scalar.copy(
                out=grouped[:].bitcast(U32).rearrange("p (e u) -> p e u", u=2),
                in_=h_pairs[:].rearrange("p u x -> p (u x)").bitcast(U32).rearrange("p (u e) -> p e u", u=2),
            )
            return grouped

        def silu_rows(chunk):
            if chunk < 3:
                acts = [tile([P, 2, EDGES], F32, "act", "act%d_%d" % (chunk, half))[:] for half in range(2)]
            else:
                act = tile([P, PACK, EDGES], F32, "act", "act%d" % chunk)
                acts = [act[:, 0:2, :], act[:, 2:4, :]]
            for low in (0, 2):
                nc.scalar.activation(acts[low // 2], sums(chunk, [low, low + 1], "a_bank%d" % (low // 2))[:], SILU)
            return acts

        def scale_rows(chunk, act, slices=range(PACK), h_rows=None):
            if h_rows is None:
                h_rows = tile([P, PACK, EDGES], BF16, "h_rows", "h_rows%d" % chunk)
            for t in slices:
                nc.scalar.activation(h_rows[:, t, :], act[t // 2][:, t % 2, :], COPY, scale=sm_sb[:, t : t + 1])
            return h_rows

        def group_rows(chunk, h_rows):
            grouped = keep.tile([P, EDGES * PACK], BF16, name="h_grouped", tag="behind_h%d" % chunk, align_bytes=64)
            nc.scalar.copy(
                out=grouped[:].rearrange("p (e f t) -> p e t f", f=4, t=PACK),
                in_=h_rows[:].rearrange("p t (e f) -> p e t f", f=4),
            )
            return grouped

        def quantise_h(chunk, grouped):
            nc.vector.quantize_mx(
                out=h_codes[:, edges_of(chunk)].bitcast(FP8X4), scales=h_scales[:, edges_of(chunk)], in_=grouped[:]
            )

        def messages(i, edges, bank_name, tag=None):
            name = "y%d_%d" % (i, edges.start)
            y = tile([P, edges.stop - edges.start], F32, name, tag or name)
            width = min(edges.stop - edges.start, BANK)
            for start in range(edges.start, edges.stop, width):
                bank = psum.tile([P, width], F32, name=bank_name)
                nc.tensor.matmul_mx(
                    out=bank[:],
                    lhsT=wd_codes[:, TURNS[i], :].bitcast(FP8X4),
                    lhsT_scale=wd_scales[:, TURNS[i], :],
                    rhs=h_codes[:, start : start + width].bitcast(FP8X4),
                    rhs_scale=h_scales[:, start : start + width],
                    start=True,
                    stop=True,
                )
                nc.scalar.copy(out=y[:, start - edges.start : start - edges.start + width], in_=bank[:])
            return y

        def scatter(i, edges, y):
            nc.vector.tensor_tensor(pages[i][:].indirect(entries(TARGET, edges)), y[:], wgo_sb[:, edges], MULT)

        def send(i, edges, bank_name, tag=None):
            scatter(i, edges, messages(i, edges, bank_name, tag))

        def deal_words(end):
            nc.scalar.copy(
                out=w_codes[:, end].bitcast(U32).rearrange("p t m -> p m t"),
                in_=w_raw[end][:].bitcast(U32).rearrange("p (m t) -> p m t", t=PACK),
            )

        deal_words(SOURCE)
        gather_scales([(SOURCE, range(0, 4)), (TARGET, range(0, 2))], "first_scales")
        gather_words([(SOURCE, range(0, 1))], "behind_first_sums")
        deal_words(TARGET)
        for half in range(2):
            slices = w_plane[:].rearrange("p (m t) -> p t m", t=PACK)[:, 2 * half : 2 * half + 2, :]
            nc.gpsimd.tensor_copy(out=w_scales[half][:], in_=slices)

        gather_words([(TARGET, range(0, 1)), (SOURCE, range(1, 4)), (TARGET, range(1, 3))], "later_words")
        wd_grouped = [
            keep.tile([P, 2, P, PACK], BF16, name="wd_grouped%d" % u, tag="behind_wd%d" % u, align_bytes=64) for u in range(2)
        ]
        for u in range(2):
            nc.vector.tensor_copy(
                out=wd_grouped[u][:].rearrange("p i m t -> p m t i"),
                in_=wd_raw[:].rearrange("p t (m i) -> p m t i", i=PACK)[:, :, :, 2 * u : 2 * u + 2],
            )
        for u in range(2):
            nc.vector.quantize_mx(
                out=wd_codes[:, 2 * u : 2 * u + 2, :].rearrange("p i m -> p (i m)").bitcast(FP8X4),
                scales=wd_scales[:, 2 * u : 2 * u + 2, :].rearrange("p i m -> p (i m)"),
                in_=wd_grouped[u][:].rearrange("p i m t -> p (i m t)"),
            )
        h_codes = keep.tile([P, J], U32, name="h_codes", tag="behind_wd0", align_bytes=64)

        quantise_h(0, activate_first())
        gather_words([(TARGET, range(3, 4))], "behind_h0")
        gather_scales([(TARGET, range(2, 4))], "behind_wd1")
        pages.append(keep.tile([P, T], F32, name="page2", tag="behind_gathers", align_bytes=64))
        nc.gpsimd.memset(pages[2][:].bitcast(I32), 0)
        pages.append(pages[0])
        act = silu_rows(1)
        send(0, edges_of(0), "y_first")
        rows = scale_rows(1, act, range(2))
        send(1, edges_of(0), "y_other", "second0")
        scale_rows(1, act, range(2, PACK), rows)
        quantise_h(1, group_rows(1, rows))
        send(2, edges_of(0), "y_other", "third0")
        act = silu_rows(2)
        rows = scale_rows(2, act, range(2))
        send(0, edges_of(1), "y_first", "first1")
        send(1, edges_of(1), "y_other", "second1")
        scale_rows(2, act, range(2, PACK), rows)
        quantise_h(2, group_rows(2, rows))
        send(2, edges_of(1), "y_other", "third1")
        rows = scale_rows(3, silu_rows(3))
        send(0, edges_of(2), "y_first", "act3")
        quantise_h(3, group_rows(3, rows))
        send(1, edges_of(2), "y_other", "h_rows3")
        send(0, edges_of(3), "y_first")
        send(1, edges_of(3), "y_other")
        send(2, edges_of(2, 2), "a_bank0")
        last_messages = messages(3, slice(0, J), "a_bank1")

        out_rows = out_0.rearrange("(p i) t -> i p t", i=PACK)
        pairs = keep.tile([P, T * PACK], BF16, name="pairs", align_bytes=64)

        def paired(cols):
            return pairs[:, cols.start * PACK : cols.stop * PACK]

        def round_into_pairs(i, cols, copy=nc.scalar.copy):
            copy(
                out=paired(cols).rearrange("p (b u c v) -> p b u c v", u=2, c=BLOCK, v=2)[:, :, TURNS[i] // 2, :, TURNS[i] % 2],
                in_=pages[i][:, cols].rearrange("p (b c) -> p b c", c=BLOCK),
            )

        for i in range(PACK - 1):
            nc.sync.dma_start(out=out_rows[TURNS[i]], in_=pages[i][:])
            round_into_pairs(i, slice(0, T))
        scatter(PACK - 1, slice(0, J), last_messages)
        nc.sync.dma_start(out=out_rows[PACK - 1], in_=pages[PACK - 1][:])

        out_plane = keep.tile([P, GROUP], U8, name="out_plane", align_bytes=64)
        out_codes = [keep.tile([P, GROUP], I32, name="out_codes%d" % g, align_bytes=64) for g in range(T // GROUP)]
        out_words = words_of(out_1)

        def interleave(cols):
            grouped = keep.tile([P, (cols.stop - cols.start) * PACK], BF16, name="grouped%d" % cols.start, align_bytes=64)
            if cols.start >= VECTOR_COLUMNS:
                round_into_pairs(PACK - 1, cols)
            move, word = (nc.vector.tensor_copy, I32) if cols.start < T - SCALAR_COLUMNS else (nc.scalar.copy, U32)
            move(
                out=grouped[:].bitcast(word).rearrange("p (b c u) -> p b c u", c=BLOCK, u=2),
                in_=paired(cols).bitcast(word).rearrange("p (b u c) -> p b c u", c=BLOCK, u=2),
            )
            return grouped

        def quantise_out(cols, grouped):
            g = cols.start // GROUP
            inside = slice(cols.start - g * GROUP, cols.stop - g * GROUP)
            nc.vector.quantize_mx(
                out=out_codes[g][:, inside].bitcast(FP8X4), scales=out_plane[4 * g :, inside], in_=grouped[:]
            )
            if g == T // GROUP - 1:
                nc.sync.dma_start(out=out_words[:, cols], in_=out_codes[g][:, inside])
            elif inside.stop == GROUP:
                nc.sync.dma_start(out=out_words[:, g * GROUP : (g + 1) * GROUP], in_=out_codes[g][:])

        pieces = [slice(sum(WIDTHS[:k]), sum(WIDTHS[: k + 1])) for k in range(len(WIDTHS))]
        for cols in pieces[:2]:
            round_into_pairs(PACK - 1, cols, nc.vector.tensor_copy)
        ahead = interleave(pieces[0])
        for k, cols in enumerate(pieces):
            current = ahead
            if k + 1 < len(pieces):
                ahead = interleave(pieces[k + 1])
            quantise_out(cols, current)
        for quad in range(QUADS):
            (nc.scalar if quad % 2 else nc.sync).dma_start(
                out=out_2[0, 4 * quad : 4 * quad + 4, :].bitcast(I32).rearrange("s (g c) -> g s c", g=T // GROUP),
                in_=out_plane[32 * quad : 32 * quad + 16, :].bitcast(I32),
            )
